import numpy as np, ml_dtypes
CORES = [16,17,18,19,32,33,34,35]
N = 8
BF = ml_dtypes.bfloat16
def gentries(a):
    return np.ascontiguousarray(a.reshape(8, 16, -1).transpose(0, 2, 1)).reshape(8, -1)
def gtable(e):
    e = np.asarray(e); return np.ascontiguousarray(e.reshape(8, -1, 16).transpose(0, 2, 1)).reshape(128, -1).astype(np.int32)
W, P, M, L, TV = 4096, 128, 32, 3, 3
def parts(rng):
    X = rng.integers(0, 256, (N, 8, 16, W))
    cen = rng.integers(0, 256, (N, 8, 16, 32)); pick = rng.integers(0, 32, (N, 8, 1, W))
    near = np.clip(np.take_along_axis(cen, pick, 3) + rng.integers(-20, 21, (N, 8, 16, W)), 0, 255)
    X[:, 1::2] = near[:, 1::2]
    Q = rng.integers(0, W, (N, 8, 16, W)); R = rng.integers(0, W, (N, 8, 16, P))
    R = np.where(rng.random((N, 8, 1, P)) < 0.0625, R[:, :, :1], R)
    return X, Q, R, rng.integers(1, 256, (N, 8, 16, 1)), rng.integers(0, 2048, (N, 8, M))
def pack(X, Q, R, w, ka):
    return {"xf": np.ascontiguousarray(X.reshape(N, 128, W)).astype(np.float32).astype(BF), "pa": np.ascontiguousarray(Q.reshape(N, 128, W)).astype(np.int32),
            "rp": np.ascontiguousarray(R.reshape(N, 128, P)).astype(np.int32), "wt": np.ascontiguousarray(w.reshape(N, 128, 1)).astype(np.int32), "kap": np.stack([gtable(a) for a in ka])}
def setup_inputs(rng):
    return pack(*parts(rng))
def setup_inputs_corners(rng):
    X, Q, R, w, ka = parts(rng); n = np.arange(W)[None, :]; k = np.arange(16)[:, None]; turn = int(rng.integers(0, 8))
    for a in range(N):
        for g in range(8):
            kind = (a + g + turn) % 8
            if kind == 0: Q[a, g] = n; w[a, g] = 255
            if kind == 1: Q[a, g] = 0; R[a, g, ::2] = 0
            if kind == 2: Q[a, g] = W - 1; R[a, g, 1::2] = W - 1
            if kind == 3: X[a, g] = int(rng.choice(np.array([0, 255, 100])))
            if kind == 4: ka[a, g] = ka[a, g, :1]
            if kind == 5: w[a, g] = 1; ka[a, g] = 0; ka[a, g, M - 1] = 2047
            if kind == 6: R[a, g] = R[a, g, :, :1]
            if kind == 7:
                R[a, g] = (R[a, g, :1] + k) & (W - 1); Q[a, g] = (n + k - 15) & (W - 1); X[a, g, :, 1::2] = X[a, g, :, ::2]
    q = int(rng.integers(0, N)); R[q] = R[q][:, :1].copy()
    return pack(X, Q, R, w, ka)
def setup_inputs_crowd(rng):
    X, Q, R, w, ka = parts(rng); o = rng.permutation(N); H = W // 4; B = W // P; hit = np.zeros((N, 8, P), bool)
    for a in range(N):
        for g in range(8):
            kind = int(rng.integers(0, 4)); hit[a, g] = (True, True, False, False)[kind]
            if kind == 1: hit[a, g, rng.integers(0, P)] = False
            if kind == 2: hit[a, g] = rng.random(P) < 0.5
    hit[o[0]] = True; hit[o[1]] = True; hit[o[1], rng.integers(0, 8), rng.integers(0, P)] = False
    hit[o[2]] = False; hit[o[3]] = False; hit[o[3], rng.integers(0, 8), rng.integers(0, P)] = True
    many = np.add.reduce(hit.reshape(N, 8 * P).astype(np.int64), axis=1); t = (int(o[2]) + 1) % N
    for g in range(8):
        for d in range(N):
            a = (t + d) % N; v = rng.integers(60, 190, 16); s = v + rng.choice(np.array([-50, 50]), 16); col = rng.permutation(W); plain = col[:H]
            if d == N - 1:
                plain, loc = keep
                X[a, g][:, plain] = v[:, None]; X[a, g][:, loc] = v
                R[a, g] = plain[rng.integers(0, H, (16, P))]; R[a, g, 1] = loc
                continue
            us = int(np.add.reduce(w[a, g, :, 0] * s)) & (W - 1); uv = int(np.add.reduce(w[a, g, :, 0] * v)) & (W - 1)
            z = ((us * us) >> 5) + int(ka[a, g, 0]) * us; c = z & (W - 1); c1 = (z + int(many[a])) & (W - 1)
            rest = col[H:]; rest = rest[(rest % B != us % B) & (rest % B != uv % B) & (rest != c) & (rest != c1)]; loc = int(rest[0])
            if d == 0: keep = (plain, loc)
            X[a, g][:, plain] = v[:, None]; X[a, g][:, c] = v; X[a, g][:, c1] = v; X[a, g][:, loc] = s; Q[a, g, 0, c] = plain[0]; Q[a, g, 0, c1] = plain[0]
            R[a, g] = plain[rng.integers(0, H, (16, P))]; R[a, g, 1] = np.where(hit[a, g], loc, R[a, g, 1])
    return pack(X, Q, R, w, ka)
def setup_inputs_ends(rng):
    X = 255 * rng.integers(0, 2, (N, 8, 16, W)); rec = 255 * rng.integers(0, 2, (N, 8, 1, W)); Q = (W - 1) * rng.integers(0, 2, (N, 8, 16, W))
    w = 1 + 254 * rng.integers(0, 2, (N, 8, 16, 1)); ka = 2047 * rng.integers(0, 2, (N, 8, M)); ka[:, :, 0] = 0; ka[:, :, M - 1] = 2047
    lo = (W - 1) * rng.integers(0, 2, (N, 8, 1, P))
    for a in range(N):
        for g in range(8): lo[a, g, 0, P - 1] = 0 if (a + g + 2) % 4 in (0, 1) else W - 1
    hi = W - 1 - lo; k = np.arange(16)[:, None]
    kind = rng.integers(0, 4, (N, 8, 1, P)); kind[..., P - 1] = 2; q = rng.integers(0, 16, (N, 8, 1, P))
    R = (W - 1) * rng.integers(0, 2, (N, 8, 16, P))
    R = np.where(kind == 1, np.where(k <= q, lo, hi), R); R = np.where(kind == 2, np.where(k == 1, hi, lo), R); R = np.where(kind == 3, rng.integers(0, W, (N, 8, 16, P)), R)
    for a in range(N):
        for g in range(8):
            role = (a + g + 2) % 4
            if role == 0 or role == 2:
                X[a, g] = rec[a, g]; X[a, g, :, 0] = 0 if role == 0 else 255; X[a, g, :, W - 1] = 255 - X[a, g, :, 0]
                if role == 0: w[a, g] = 255
                else:
                    u = (255 * int(np.add.reduce(w[a, g, :, 0]))) & (W - 1)
                    for kk in (0, 2047):
                        c = (((u * u) >> 5) + kk * u) & (W - 1)
                        if 0 < c < W - 1: X[a, g, :, c] = 255; Q[a, g, :, c] = W - 1
            else:
                o = rng.permutation(16); w[a, g, o[0], 0] = 255; w[a, g, o[1], 0] = 1; w[a, g, o[2], 0] = 1; top = W - 1 if role == 1 else 0
                v = np.zeros(16, np.int64); v[o[:3]] = 255; X[a, g, :, top] = v; X[a, g, :, W - 1 - top] = 255 - v
                if role == 1: ka[a, g] = 0; ka[a, g, M - 1] = 2047
                else:
                    f = 2 if g < 4 else 3; u = W - 1
                    ka[a, g, :f] = 0; ka[a, g, f] = 2047; ka[a, g, f + 1] = 1
                    for kk, i in ((0, -1), (2047, int(o[3])), (1, int(o[4]))):
                        c = (((u * u) >> 5) + kk * u) & (W - 1)
                        X[a, g, :, c] = v; Q[a, g, 0, c] = W - 1
                        if i >= 0: X[a, g, i, c] = 255 - v[i]
    return pack(X, Q, R, w, ka)
def setup_inputs_spread(rng):
    X, Q, R, w, ka = parts(rng); e = rng.choice(np.array([1, 2, 4, 8]), (N, 8, 1, 1)); back = rng.random((N, 8, 1, 1)) < 0.5
    X = np.minimum((np.exp2(8 * rng.random((N, 8, 1, W))) * np.exp2(-3 * rng.random((N, 8, 16, 1))) * (0.5 + rng.random((N, 8, 16, W)))).astype(np.int64), 255)
    Q = np.minimum((W * rng.random((N, 8, 16, W)) ** e).astype(np.int64), W - 1); Q = np.where(back, W - 1 - Q, Q)
    R = np.minimum((W * rng.random((N, 8, 16, P)) ** e[:, ::-1]).astype(np.int64), W - 1); R = np.where(back, R, W - 1 - R)
    w = np.minimum(np.exp2(8 * rng.random((N, 8, 16, 1))).astype(np.int64), 255); ka = np.minimum(np.exp2(11 * rng.random((N, 8, M))).astype(np.int64) - 1, 2047)
    return pack(X, Q, R, w, ka)
def brink(rng, X, Q, R, w, ka):
    pl = 4093 & (W - 1); v = rng.integers(60, 190, 16); w[0] = 16; w[1] = 1; ka[0] = 1929; ka[1] = 815
    goal = [4081 & (W - 1), 5]
    cs = [(((goal[m] * goal[m]) >> 5) + int(ka[m]) * goal[m]) & (W - 1) for m in range(2)]
    col = rng.permutation(W); col = col[(col != pl) & (col != cs[0]) & (col != cs[1]) & (col > 0) & (col < W - 1)][:5]
    X[:, pl] = v
    for m in range(2):
        s = v + rng.choice(np.array([-50, 50]), 16); rest = (goal[m] - int(np.add.reduce((w[:, 0] * s)[2:]))) & (W - 1); s[0] = rest >> 4; s[1] = rest & 15
        X[:, col[m]] = s; X[:, cs[m]] = v; Q[0, cs[m]] = pl; R[:, m::4] = pl; R[1, m::4] = col[m]
    X[:, col[2]] = 0; X[:, col[3]] = 255; X[:, col[4]] = 255; X[int(rng.integers(0, 16)), col[4]] = 254
    for j, way in ((2, (4, 2, 2, 3)), (3, (2, 4, 3, 2))):
        for k in range(4): R[k + 1, j::4] = col[way[k]]
def setup_inputs_ties(rng):
    X, Q, R, w, ka = parts(rng); turn = int(rng.integers(0, 8))
    for a in range(N):
        for g in range(8):
            if (a + g + turn) % 8 == 7:
                brink(rng, X[a, g], Q[a, g], R[a, g], w[a, g], ka[a, g])
                continue
            top = int(rng.choice(np.array([1, 2, 3]))); o = rng.permutation(16)[:3]; v = rng.integers(0, 252, 16)
            X[a, g] = v[:, None]; X[a, g, o] = v[o][:, None] + rng.integers(0, top + 1, (3, W))
    return pack(X, Q, R, w, ka)
def check_inputs(d):
    bad = []
    for k, lo, hi in (("xf", 0, 255), ("pa", 0, W - 1), ("rp", 0, W - 1), ("wt", 1, 255), ("kap", 0, 2047)):
        v = np.asarray(d[k]).astype(np.float64)
        if not np.all((v >= lo) & (v <= hi)): bad.append("range of " + k)
        elif not np.all(v == np.floor(v)): bad.append("whole numbers in " + k)
    return bad
def reference(xf, pa, rp, wt, kap):
    X = xf.astype(np.float32).astype(np.int32).reshape(N, 8, 16, W); Q = pa.astype(np.int64).reshape(N, 8, 16, W); R = rp.astype(np.int64).reshape(N, 8, 16, P)
    w = wt.astype(np.int64).reshape(N, 8, 16, 1); ka = np.stack([gentries(a) for a in kap]).astype(np.int64); A = np.zeros(N, np.int64)
    k = np.arange(16)[:, None]; B = W // P
    for v in range(TV):
        S = np.roll(R, v, axis=0)
        x = np.take_along_axis(X, S.reshape(N, 8, 1, 16 * P), 3).reshape(N, 8, 16, 16, P)
        D = np.add.reduce(np.abs(x[:, :, :, 2:16 - L] - x[:, :, :, 1:15 - L]), axis=2)
        p = 1 + np.argmax(D, axis=2)
        xt = [np.take_along_axis(x, (p + j)[:, :, None, None, :], 3)[:, :, :, 0] for j in range(L + 1)]
        u = np.add.reduce(w * xt[0], axis=2) & (W - 1)
        c = (((u * u) >> 5)[:, :, None] + ka[..., None] * u[:, :, None] + A[:, None, None, None]) & (W - 1)
        anc = np.take_along_axis(Q, c.reshape(N, 8, 1, M * P), 3).reshape(N, 8, 16, M, P)
        b = np.take_along_axis(anc, (p - 1)[:, :, None, None, :], 2)[:, :, 0]
        pk = p[:, :, None]
        cc = np.concatenate([np.take_along_axis(S, pk, 2), c], axis=2); bb = np.concatenate([np.take_along_axis(S, pk - 1, 2), b], axis=2)
        Xc = np.take_along_axis(X, cc.reshape(N, 8, 1, -1), 3).reshape(N, 8, 16, M + 1, P); Xb = np.take_along_axis(X, bb.reshape(N, 8, 1, -1), 3).reshape(N, 8, 16, M + 1, P)
        E = np.zeros((N, 8, M + 1, P), np.int64)
        for j in range(1, L + 1):
            E = E + np.add.reduce(np.abs(Xc + j * (Xc - Xb) - xt[j][:, :, :, None, :]), axis=2)
        m = np.argmin(E, axis=2)
        win = np.take_along_axis(cc, m[:, :, None], 2)
        pre = np.take_along_axis(anc, np.maximum(m - 1, 0)[:, :, None, None, :], 3)[:, :, :, 0]
        late = (((S * win) >> 5) + S + 37 * k) & (W - 1)
        new = np.where(k < pk, pre, np.where(k == pk, win, np.where(k > pk + L, late, S)))
        S2 = np.where((m > 0)[:, :, None], new, S)
        mid = (np.take_along_axis(Xc, m[:, :, None, None, :], 3)[:, :, :, 0] + xt[1]) >> 1
        n = np.broadcast_to((B * np.arange(P) + (u & (B - 1)))[:, :, None], (N, 8, 16, P))
        np.put_along_axis(Q, n, S2, 3); np.put_along_axis(X, n, mid, 3)
        A = np.add.reduce((m > 0).astype(np.int64).reshape(N, 8 * P), axis=1)
        R = np.roll(S2, -v, axis=0)
    return {"yr": R.reshape(N, 128, P).astype(np.float32), "yq": np.add.reduce((k + 1) * Q, axis=2).astype(np.float32), "yx": np.add.reduce((k + 1) * X, axis=2).astype(np.float32)}

@@ -1,0 +1,674 @@
+from concourse.mybir import AluOpType, ActivationFunctionType
+
+ADD, SUB, MUL, MAX, MIN = AluOpType.add, AluOpType.subtract, AluOpType.mult, AluOpType.max, AluOpType.min
+EQ, NE, GT, GE, LT = AluOpType.is_equal, AluOpType.not_equal, AluOpType.is_gt, AluOpType.is_ge, AluOpType.is_lt
+AND, SHR = AluOpType.bitwise_and, AluOpType.arith_shift_right
+IDENT, ABS, SQUARE, SIGN = (ActivationFunctionType.Identity, ActivationFunctionType.Abs,
+                            ActivationFunctionType.Square, ActivationFunctionType.Sign)
+F32, BF, F16, I32, U16 = "float32", "bfloat16", "float16", "int32", "uint16"
+W, VISITS = 4096, 3
+SEND_ENGINES = 8
+ON_SCALAR = (3, 7)
+ITEMS = [(0, 0), (0, 1), (0, 2), (1, 0), (1, 1), (1, 2), (2, 0), (3, 0), (2, 1), (3, 1), (2, 2), (3, 2),
+         (4, 0), (4, 1), (4, 2), (5, 0), (5, 1), (5, 2), (6, 0), (7, 0), (6, 1), (7, 1), (6, 2), (7, 2), (8, 0), (8, 1), (8, 2)]
+AFTER = {1: ["q4"], 3: ["q5"], 5: ["b2", "x2"], 6: ["q6"], 8: ["q7"], 10: ["b3"], 11: ["x3", "tab"],
+         12: ["T1"], 13: ["ct"], 14: ["M1"], 15: ["Tt"], 16: ["MM"]}
+AHEAD = 3
+CYC, PE_CYC, GATHER, SCATTER, HANDOVER, DMA_RATE, PASSES = 1.04, 0.52, 1.5, 3.5, 80.0, 250.0, 8
+
+_SB = {
+    "X": (2 * W, BF), "Qi": (W, I32), "Qf": (W + 8, F32), "It": (W + 8, F32), "Y": (W, F32),
+    "Ri": (128, I32), "wI": (4, I32), "kI": (4, I32), "wF": (1, F32), "kF": (2, F32),
+    "R0": (128, U16), "R1": (128, U16), "R2": (128, U16), "Rfin": (128, F32),
+    "S0": (128, U16), "S1": (128, U16), "S2": (128, F32), "Rf": (128, F32),
+    "pI": (16, I32), "pJ": (16, I32), "r16": (1, F32), "g16": (1, F32), "cols": (32, F32),
+    "ybias": (1, F32), "Acol": (1, F32), "cnt": (1, F32),
+    "tM": (144, BF), "tB": (72, BF), "tA": (520, BF), "tD": (16, F32), "tE": (128, F32), "tI": (48, I32), "tJ": (32, I32),
+    "sel": (144, F16), "idn": (256, BF), "Wl": (384, BF), "bdb": (48, BF), "bdh": (48, F16), "diag": (128, BF),
+    "eu": (8, F32), "ep": (72, F32), "cp": (72, F16), "lhc": (128, F16), "rowc": (384, BF), "onf": (128, F32),
+    "eg": (272, BF), "cg": (272, BF), "eo": (32, BF), "co": (16, BF), "c1": (128, F32), "ce": (264, F32),
+    "cu": (128, BF), "l11": (8, U16), "lg": (8, U16), "l8": (16, U16), "lc": (18, U16),
+    "cm": (272, F32), "krep": (256, F32), "kh": (256, F16), "bdf": (128, F16),
+    "OH": (16, BF), "ML": (16, F32), "C1": (16, F32), "C2": (16, F32), "C3": (16, F32), "C4": (16, F32),
+    "nq": (16, I32), "KQ": (128, F16), "KX": (128, BF), "q16": (1024, F16),
+    "x": (2048, BF), "ab": (1408, BF), "run1": (128, F32), "new": (128, F32), "sc3": (128, F32), "lhU": (128, F32),
+    "uP": (16, I32), "uI": (8, I32), "sq": (16, F32), "sI": (8, I32), "z1": (256, F32), "zI": (256, I32),
+    "cX": (264, I32), "c16": (256, U16), "off": (72, U16), "msk": (512, BF), "Qs": (W, F16), "b16": (256, U16),
+    "AB": (2 * (W + 128), BF), "x5": (640, BF), "tsum": (128, F16), "t3": (1536, BF), "Mx": (3 * (W + 128), F16),
+    "ctab": (272, F32), "T1": (128, F32), "Tt": (256, F32), "M1": (128, F32), "MM": (128, F32), "MLg": (128, F32),
+    "runE": (264, F32), "mP": (8, I32), "mI": (8, I32), "lhM": (128, BF), "lhS": (128, BF), "runG": (264, F32),
+    "lf": (24, F32), "l16": (24, U16), "h1": (128, F32), "h2": (128, F32), "h3": (128, F32), "h4": (128, I32), "nI": (128, I32),
+    "n1": (16, I32), "n2": (16, I32), "n16": (16, U16), "ms": (128, F32), "mf": (128, I32), "mb": (256, BF),
+    "nF": (128, F16), "Yn": (128, F32),
+}
+_PS = ["pA0", "pA1", "pA2", "pA3", "pD", "pU", "pS", "pB"]
+SCRATCH = {k: ("sbuf", [128, v[0]], v[1]) for k, v in _SB.items()}
+SCRATCH.update({k: ("psum", [128, 512], F32) for k in _PS})
+SEMAPHORES = ["cV", "cS", "cP", "cG", "ldR", "ldW", "ldK", "ldX0", "ldX1", "ldX2", "ldX3", "ldQ0", "ldQ1", "ldQ2", "ldQ3",
+              "arr0", "arr1", "arr2", "sent", "stR", "stQ", "stX"]
+
+
+_ORDER, _WAITS = [], []
+
+
+def plan(ops, clash):
+    n_ops = len(ops)
+    pred, succ, seen, sends = [set() for _ in ops], [[] for _ in ops], {}, []
+    last_dma = []
+    for n, o in enumerate(ops):
+        names = {r[0] for r in o["r"] + o["w"]}
+        for m in {m for nm in names for m in seen.get(nm, [])}:
+            if clash(ops[m], o):
+                pred[n].add(m)
+        if o["q"] is None:
+            pred[n].add(sends[-1])
+        if o["sem"] == "remote":
+            sends.append(n)
+        elif o["bytes"] and not o["r"]:
+            pred[n].update(last_dma[-1:])
+            last_dma.append(n)
+        for nm in names:
+            seen.setdefault(nm, []).append(n)
+    unit = ["D" if o["bytes"] else o["q"] for o in ops]
+    cost = [o["bytes"] / DMA_RATE if o["bytes"] else o["cost"] for o in ops]
+    pred = [[(m, 0.0 if unit[m] == unit[n] and unit[n] in "PD" else ops[m]["lat"] + HANDOVER) for m in p] if ops[n]["q"] else
+            [(m, ops[m]["lat"]) for m in p] for n, p in enumerate(pred)]
+    for n, p in enumerate(pred):
+        for m, lag in p:
+            succ[m].append((n, lag))
+
+    def place(order, before):
+        busy, end = {}, [0.0] * n_ops
+        for n in order:
+            t = max([end[m] + lag for m, lag in before[n]] + [0.0])
+            spans = busy.setdefault(unit[n], [])
+            k = bisect(spans, t)
+            while k < len(spans) and spans[k][0] < t + cost[n]:
+                t = max(t, spans[k][1])
+                k += 1
+            spans.insert(k, (t, t + cost[n]))
+            end[n] = t + cost[n]
+        return end
+
+    def bisect(spans, t):
+        lo, hi = 0, len(spans)
+        while lo < hi:
+            mid = (lo + hi) // 2
+            lo, hi = (mid + 1, hi) if spans[mid][1] <= t else (lo, mid)
+        return lo
+
+    end = place(range(n_ops), pred)
+    best = end
+    for _ in range(PASSES):
+        back = place(sorted(range(n_ops), key=lambda n: (-end[n], -n)), succ)
+        end = place(sorted(range(n_ops), key=lambda n: (-back[n], n)), pred)
+        best = end if max(end) < max(best) else best
+    return last_dma + sorted(set(range(n_ops)) - set(last_dma), key=lambda n: (best[n] - cost[n], best[n], n))
+
+
+def rank_program(g, core, T, topo):
+    rank = T.rank_of(core)
+    if rank is None:
+        return
+    n_ranks = len(T.cores)
+    Q = {"V": g.vector, "S": g.scalar, "P": g.tensor, "G": g, "Y": g.sync}
+    ops = []
+
+    def a(name, lo=0, hi=None, st=1, rows=128, half=None):
+        hi = SCRATCH[name][1][1] if hi is None else hi
+        cols = slice(lo, hi) if st == 1 else slice(lo, hi, st)
+        p0, p1 = (0, rows) if half is None else (64 * half, 64 * half + 64)
+        return (T[name][p0:p1, cols], [(name, lo, hi, p0, p1)], len(range(lo, hi, st)), SCRATCH[name][2] in (BF, F16, U16))
+
+    def ind(win, off):
+        return (win[0].indirect(off[0]), win[1] + off[1], 0, False)
+
+    def cost(out, x, rate=None):
+        rate = GATHER if not x[2] else rate or (0.5 if out[3] and x[3] else 1.0)
+        return 60.0 + out[2] * rate * CYC
+
+    def ap(x):
+        return x[0] if isinstance(x, tuple) else x
+
+    def rg(*xs):
+        return [r for x in xs if isinstance(x, tuple) for r in x[1]]
+
+    def op(q, fn, reads, writes, ns, sem=None, val=None, lat=0.0, nbytes=0, adds=False):
+        ops.append({"q": q, "fn": fn, "r": reads, "w": writes, "sem": sem, "val": val, "cost": ns, "lat": lat,
+                    "bytes": nbytes, "adds": adds})
+
+    def ts(out, x, s1, o0, s2=None, o1=None):
+        if o1 is None:
+            op("V", lambda: g.vector.tensor_scalar(out[0], x[0], ap(s1), None, o0), rg(x, s1), rg(out), cost(out, x))
+        else:
+            op("V", lambda: g.vector.tensor_scalar(out[0], x[0], ap(s1), ap(s2), o0, o1), rg(x, s1, s2), rg(out), cost(out, x))
+
+    def tt(out, x, y, o):
+        op("V", lambda: g.vector.tensor_tensor(out[0], x[0], y[0], o), rg(x, y), rg(out),
+           cost(out, x, 1.0 if x[1][0][0] in _PS else 2.0))
+
+    def cp(out, x):
+        op("V", lambda: g.vector.tensor_copy(out[0], x[0]), rg(x), rg(out), cost(out, x))
+
+    def scatter(win, off, x):
+        op("V", lambda: g.vector.tensor_copy(win[0].indirect(off[0]), x[0]), rg(x, off), rg(win), cost(x, x, SCATTER))
+
+    def scan(out, d0, d1, init, o0, o1):
+        op("V", lambda: g.vector.tensor_tensor_scan(out[0], d0[0], d1[0], init, o0, o1), rg(d0, d1), rg(out), cost(out, d0))
+
+    def fill(out, c):
+        op("V", lambda: g.vector.memset(out[0], c), [], rg(out), cost(out, out))
+
+    def act(out, x, f=IDENT, bias=0.0, scale=1.0, acc=None):
+        op("S", lambda: g.scalar.activation(out[0], x[0], f, bias=ap(bias), scale=scale, accum_out=ap(acc)),
+           rg(x, bias), rg(out, acc), 10.0 + cost(out, x, 1.0))
+
+    def mm(out, l, r, start, stop):
+        op("P", lambda: g.tensor.matmul(out[0], l[0], r[0], start, stop), rg(l, r), rg(out),
+           10.0 + max(min(64, l[2]), r[2]) * PE_CYC * (1 if l[3] else 4), lat=60.0, adds=not (start or stop))
+
+    def iota(out, pat, base=0, cmul=0):
+        if SCRATCH[out[1][0][0]][2] == I32:
+            op("G", lambda: g.iota(out[0], pat, base, cmul), [], rg(out), 70.0 + cost(out, out, 2.0))
+        else:
+            op("G", lambda: g.iota(out[0], pat, base, cmul, allow_small_or_imprecise_dtypes=True), [], rg(out),
+               70.0 + cost(out, out, 2.0))
+
+    def keep(out, x, pat, cmp_, other, base):
+        op("G", lambda: g.affine_select(out[0], x[0], pat, cmp_, other, base, 0), rg(x), rg(out), 110.0 + cost(out, out, 2.0))
+
+    def dma(q, out, x, sem, nbytes):
+        op(q, lambda: Q[q].dma_start(ap(out), ap(x)), rg(x), rg(out), 100.0, sem, 16, 1800.0, nbytes)
+
+    def send(src, dst_name, to_rank, v):
+        to = T.cores[to_rank]
+        rid, pid, _ = topo.addr(to)
+        engs = topo.engines(core, to)[:SEND_ENGINES]
+        m = sum(1 << e for e in engs)
+        op("G", lambda: g.remote_dma(T[dst_name][:, :], src[0], T.sem["arr%d" % v], T.sem.sent, pid, rid, m), rg(src), [],
+           300.0, "remote", 0, 2500.0)
+        return len(engs)
+
+    def arrive(name, from_rank, v):
+        n = len(topo.engines(T.cores[from_rank], core)[:SEND_ENGINES])
+        op(None, None, [], rg(a(name)), 0.0, "arr%d" % v, n)
+
+    dma("S", a("Ri"), T.rp[:, :], "ldR", 65536)
+    dma("Y", a("wI", 0, 1), T.wt[:, :], "ldW", 512)
+    dma("S", a("kI", 0, 2), T.kap[:, :], "ldK", 1024)
+    dma("Y", a("X", 0, 2048), T.xf[:, 0:2048], "ldX0", 1 << 19)
+    dma("S", a("X", 2048, W), T.xf[:, 2048:W], "ldX1", 1 << 19)
+    for j in range(4):
+        dma("Y", a("Qi", 1024 * j, 1024 * j + 1024), T.pa[:, 1024 * j:1024 * j + 1024], "ldQ%d" % j, 1 << 19)
+    for h in range(2):
+        dma("Y", a("X", W, 2 * W, half=h), T.xf[64 - 64 * h:128 - 64 * h, :], "ldX%d" % (2 + h), 1 << 19)
+
+    r16, g16 = a("r16"), a("g16")
+    pcol, npcol, p16, kgt, r1, g17, hi, sgn, p64, g64, g64b, gsw, top64, bot64, robias = (a("cols", j, j + 1) for j in range(15))
+    col, blk8 = a("tM", 15, 143), a("tB", 0, 8)
+    zrow, r5, r19 = (a("rowc", 128 * j, 128 * j + 128, rows=1) for j in range(3))
+    iota(a("pI"), [[0, 16]], 0, 1)
+    iota(a("tM"), [[1, 144]], -15)
+    iota(a("tB"), [[0, 9], [16, 8]])
+    iota(a("cu"), [[0, 8], [1, 16]])
+    iota(a("tI", 0, 8), [[16, 8]], 11)
+    iota(a("tI", 8, 16), [[1, 8]])
+    iota(a("tE", 0, 40), [[1, 5], [256, 8]], -1)
+    iota(a("tA", 0, 128), [[16, 8], [0, 16]])
+    iota(a("tA", 128, 256), [[1, 16], [0, 8]])
+    fill(a("c1"), 1.0e6)
+    fill(a("rowc", 0, 128), 0.0)
+    fill(a("rowc", 128, 256), 2.0 ** -5)
+    fill(a("rowc", 256, 384), 2.0 ** 19)
+    keep(a("c1"), a("c1"), [[0, 8], [1, 16]], GE, -1.0, -1)
+    keep(a("c1"), a("c1"), [[0, 8], [-1, 16]], GE, -1.0, 11)
+    iota(a("tA", 256, 520), [[16, 8], [0, 33]])
+    iota(a("tI", 16, 33), [[16, 17]])
+    iota(a("cg", 0, 264), [[0, 8], [2, 33]], -1)
+    iota(a("cg", 264, 272), [[0, 8]])
+    fill(a("new", 0, 1), 1.0)
+    fill(a("Acol"), -31.0 / 64)
+    fill(a("cp", 0, 32), 0.0)
+    fill(a("cX", 0, 8), W)
+    fill(a("Qf", W, W + 8), 0.0)
+    fill(a("It", W, W + 8), 0.0)
+    fill(a("eo", 8, 24), 0.0)
+    fill(a("onf"), 1.0)
+    fill(a("ce"), -1.0)
+    ts(a("pJ", 0, 1), a("pI", 0, 1), 15, AND)
+    cp(pcol, a("pI", 0, 1))
+    cp(r16, a("pJ", 0, 1))
+    tt(g16, a("pI", 0, 1), a("pJ", 0, 1), SUB)
+    ts(a("pJ"), a("pI"), 7, AND)
+    ts(hi, pcol, 64.0, GE, 64.0, MUL)
+    scales = (1, -1)
+    for j, c in enumerate(scales):
+        ts(a("idn", 128 * j, 128 * j + 128), col, pcol, EQ, float(c), MUL)
+    idn = {c: a("idn", 128 * j, 128 * j + 128) for j, c in enumerate(scales)}
+    cp(a("l8"), a("pJ"))
+    ts(npcol, pcol, -1.0, MUL, 1.0, ADD)
+    ts(p16, pcol, 16.0, MUL)
+    ts(kgt, r16, 1184.0, MUL, -2.0 ** 23, ADD)
+    ts(r1, r16, 1.0, ADD)
+    ts(g17, g16, 1.0, ADD)
+    ts(sgn, hi, -1.0 / 64, MUL, 0.5, ADD)
+    ts(p64, pcol, hi, SUB)
+    ts(g64, g16, hi, SUB)
+    ts(top64, hi, 64.0, SUB)
+    ts(bot64, hi, -1.0, MUL)
+    ts(robias, hi, (W + 128) / 64.0, MUL, r16, ADD)
+    ts(g64b, g64, 64.0, ADD)
+    ts(gsw, g64, top64, SUB)
+    ts(a("cols", 16, 24), blk8, 0.125, MUL, -7.0, ADD)
+    ts(a("sel"), a("tM"), gsw, EQ)
+    ts(a("cols", 24, 32), a("cols", 16, 24), sgn, MUL, 0.5, ADD)
+    for j, c in enumerate((2.0, -1.0, 1.0, top64, bot64)):
+        ts(a("bdb", 8 * j, 8 * j + 8), blk8, g16, EQ, c, MUL)
+    bd2, bdm1, bd1, bdtop, bdbot, bdw = (a("bdb", 8 * j, 8 * j + 8) for j in range(6))
+    for j, c in enumerate((5, 6, 1, 2, 7, 0)):
+        ts(a("Wl", 64 * j, 64 * j + 64), a("tM", 15, 79), p64, EQ, a("cols", 24 + c, 25 + c), MUL)
+    ts(a("diag"), a("cu"), r16, EQ)
+    ts(a("lhc"), a("cu"), p16, MUL, npcol, ADD)
+    ts(a("eu"), blk8, g16, EQ, 2.0 ** 25, MUL)
+    ts(a("ep"), a("tB"), g16, EQ, 32.0, MUL)
+    cp(a("l11"), a("tI", 0, 8))
+    cp(a("lg"), a("tI", 8, 16))
+    ts(a("cp", 32, 72), a("tE", 0, 40), npcol, MUL, pcol, ADD)
+    cp(a("R0"), a("Ri"))
+    ts(a("bdf"), a("tA", 0, 128), g16, EQ)
+    dk = a("tD")
+    ts(dk, a("cu", 0, 16), r16, SUB)
+    for j, (gg, c) in enumerate(((g64, 128.0), (g64b, 128.0), (g16, -128.0), (g64, 64.0), (g64b, 64.0), (g16, 64.0))):
+        ts(a("bdh", 8 * j, 8 * j + 8), blk8, gg, EQ, c, MUL)
+    ts(a("OH"), dk, 1.0, EQ)
+    ts(a("ML"), dk, 0.0, GT, 32.0, MUL)
+    ts(a("C3"), dk, -3.0, LT)
+    ts(a("C4"), dk, 0.0, EQ, 32.0, MUL)
+    ts(a("C1"), dk, 0.0, LT, 32.0, MUL)
+    ts(a("C2"), dk, 0.0, GE, 65536.0, MUL)
+    ts(a("tE", 48, 64), a("C3"), 2048.0, MUL)
+    ts(a("tE", 64, 80), a("C3"), kgt, MUL)
+    ts(a("KQ"), col, g16, EQ, r1, MUL)
+    tt(a("C1"), a("C1"), a("tE", 48, 64), ADD)
+    tt(a("C2"), a("C2"), a("tE", 64, 80), ADD)
+    ts(a("KX"), col, g17, EQ, r1, MUL)
+    ts(a("ybias"), r16, 0.0, EQ, 2048.0 * 136, MUL)
+    ts(a("eo", 0, 8), blk8, g16, EQ, 128.0, MUL)
+    ts(a("eo", 24, 32), blk8, g16, EQ, -128.0, MUL)
+    ts(a("eg", 264, 272), blk8, g16, EQ, 8192.0, MUL)
+    ts(a("nq"), a("tB", 0, 16), r16, ADD, 32.0, MUL)
+    ts(a("wF"), a("wI", 0, 1), 2.0 ** -25, MUL)
+    cp(a("kF"), a("kI", 0, 2))
+    ts(bdw, blk8, g16, EQ, a("wF"), MUL)
+    for h in range(2):
+        ts(a("kh", 128 * h, 128 * h + 128), a("tA", 128, 256), r16, EQ, a("kF", h, h + 1), MUL)
+    mm(a("pB", 0, 256), a("bdf"), a("kh"), True, True)
+
+    def late_constants():
+        ts(a("tE", 80, 97), a("tI", 16, 33), r16, ADD)
+        ts(a("eg", 0, 264), a("tA", 256, 520), g16, EQ, -2.0 ** 20, MUL)
+        ts(a("tJ", 0, 17), a("tE", 80, 97), 16.0, SUB, 1.0 / 33, MUL)
+        ts(a("tE", 80, 97), a("tE", 80, 97), 8.0, MUL)
+        ts(a("tE", 100, 117), a("tJ", 0, 17), -263.0, MUL)
+        tt(a("tE", 80, 97), a("tE", 80, 97), a("tE", 100, 117), ADD)
+        cp(a("lc", 0, 17), a("tE", 80, 97))
+        keep(a("ce"), a("ce"), [[0, 8], [1, 33]], NE, 3.0e7, 0)
+        iota(a("cm", 0, 264), [[0, 8], [-8192, 33]])
+        iota(a("cm", 264, 272), [[0, 8]])
+        iota(a("co"), [[4096, 2], [512, 8]])
+        iota(a("It", 0, 1024), [[1, 1024]], -2048)
+
+    Xw, Qw, Iw, Yw = a("X", 0, W), a("Qf"), a("It"), a("Y")
+    WB = W + 128
+    banks = [(1, 3, "V"), (4, 3, "S"), (7, 2, "V"), (9, 3, "S")]
+    y_front = [[], [2, 3], [6, 7]]
+    y_back = [[0, 1], [4, 5], []]
+    sent = 0
+
+    def conv_q(lo, hi, q):
+        if q == "S":
+            act(a("Qf", lo, hi), a("Qi", lo, hi), bias=-2048.0)
+        else:
+            ts(a("Qf", lo, hi), a("Qi", lo, hi), 2048.0, SUB)
+
+    def y_x(c, bank):
+        mm(a(bank), a("KX"), a("X", 512 * c, 512 * c + 512), True, False)
+
+    def y_q(c, bank):
+        q16 = a("q16", 512 * (c % 2), 512 * (c % 2) + 512)
+        act(q16, a("Qf", 512 * c, 512 * c + 512))
+        mm(a(bank), a("KQ"), q16, False, True)
+
+    def y_out(c, bank):
+        act(a("Y", 512 * c, 512 * c + 512), a(bank), bias=a("ybias"))
+
+    for v in range(VISITS):
+        Rn = "R%d" % v
+        if v:
+            arrive(Rn, (rank - 1) % n_ranks, v - 1)
+        mm(a("pD", 0, 128), zrow, a("cu", rows=1), True, False)
+        mm(a("pU", 0, 128), r5, a("cu", rows=1), True, False)
+        for h in range(2):
+            cp(a("x", 1024 * h, 1024 * h + 512), ind(Xw, a(Rn, 64 * h, 64 * h + 32)))
+            act(a("x", 1024 * h + 512, 1024 * h + 1024), ind(Xw, a(Rn, 64 * h + 32, 64 * h + 64)))
+            for b, (k0, nk, who) in enumerate(banks):
+                for j in range(nk):
+                    o = a("pA%d" % b, 128 * j + 64 * h, 128 * j + 64 * h + 64)
+                    mm(o, idn[1], a("x", 1024 * h + k0 + j + 1, 1024 * h + 1024, 16), True, False)
+                    mm(o, idn[-1], a("x", 1024 * h + k0 + j, 1024 * h + 1024, 16), False, True)
+        if v:
+            act(a("Yn"), a("pS", 0, 128), bias=a("ybias"))
+            act(a("mb", 128, 256), a("pS", 128, 256))
+            scatter(a("Qf", 0, W), a("n16", 0, 8), a("nF"))
+        else:
+            act(a("krep"), a("pB", 0, 256), bias=128.0)
+            late_constants()
+        for k0, nk, who in banks:
+            for k in range(k0, k0 + nk):
+                if who == "V":
+                    mm(a("pD", k, 128, 16), a("x", k + 1, 2048, 16), bdm1, False, False)
+                    mm(a("pD", k, 128, 16), a("x", k, 2048, 16), bd1, False, False)
+        for b, (k0, nk, who) in enumerate(banks):
+            dst, src = a("ab", 128 * (k0 - 1), 128 * (k0 - 1 + nk)), a("pA%d" % b, 0, 128 * nk)
+            if who == "V":
+                ts(dst, src, 0.0, MAX)
+            else:
+                act(dst, src, ABS)
+            for k in range(k0, k0 + nk):
+                mm(a("pD", k, 128, 16), a("ab", 128 * (k - 1), 128 * k), bd2 if who == "V" else bd1, False, False)
+        for k in range(1, 12):
+            mm(a("pU", k, 128, 16), a("x", k, 2048, 16), bdw, False, False)
+        mm(a("pD", 0, 8), zrow, a("cu", 0, 8, rows=1), False, True)
+        mm(a("pU", 0, 8), zrow, a("cu", 0, 8, rows=1), False, True)
+        if v == 0:
+            conv_q(0, 1024, "S")
+            conv_q(1024, 2048, "S")
+        if v:
+            scatter(a("X", W, 2 * W), a("n16", 8, 16), a("mb", 128, 256))
+        scan(a("run1"), a("pD", 0, 128), a("c1"), -1.0, MAX, MIN)
+        tt(a("new", 1, 128), a("pD", 1, 128), a("run1", 0, 127), GT)
+        mm(a("pD", 0, 72), a("lhc", rows=2), a("cp", rows=2), True, False)
+        scan(a("sc3"), a("new"), a("pU", 0, 128), 0.0, MAX, MIN)
+        tt(a("lhU"), ind(a("sc3"), a("l11")), a("diag"), MUL)
+        mm(a("pB", 0, 8), a("lhU"), a("eu"), True, True)
+        mm(a("pD", 0, 72), a("lhU"), a("ep"), False, True)
+        for h in range(2):
+            mm(a("pU", 0, 8, half=h), a("lhU", 64 - 64 * h, 128 - 64 * h), a("eu"), True, True)
+        if v:
+            scatter(Yw, a("n16", 0, 8), a("Yn"))
+        cp(a("uP", 0, 8), a("pB", 0, 8))
+        ts(a("off"), a("pD", 0, 72), -0.4961, ADD)
+        ts(a("uI"), a("uP", 0, 8), W - 1, AND)
+        act(a("sq"), ind(a("uI"), a("l8", 0, 1)), SQUARE, bias=-2048.0)
+        act(a("msk"), ind(a("OH"), a("off", 0, 32)))
+        act(a("x5"), ind(a("x"), a("off", 32, 72)))
+        if y_front[v]:
+            y_x(y_front[v][0], "pA3")
+            y_q(y_front[v][0], "pA3")
+        for j, (f, s) in enumerate(((2, 3), (1, 0))):
+            xf_, xs_ = a("x5", 128 * f, 128 * f + 128), a("x5", 128 * s, 128 * s + 128)
+            lo, up = a("idn", 0, 64), a("idn", 64, 128)
+            mm(a("pA0", 256 * j, 256 * j + 128, half=0), lo, xf_, True, True)
+            mm(a("pA0", 256 * j, 256 * j + 128, half=1), lo, xs_, True, True)
+            mm(a("pA0", 256 * j + 128, 256 * j + 256, half=0), up, xs_, True, True)
+            mm(a("pA0", 256 * j + 128, 256 * j + 256, half=1), up, xf_, True, True)
+        for j, c in enumerate((1, 1, -1)):
+            mm(a("pA1", 0, 128), idn[c], a("x5", 256 + 128 * j, 384 + 128 * j), j == 0, j == 2)
+        if y_front[v]:
+            y_x(y_front[v][1], "pD")
+            y_q(y_front[v][1], "pD")
+        keep(a("t3", 1024, 1152), a("x5", 512, 640), [[0, 128]], GE, 0.0, 0)
+        for j in range(2):
+            act(a("t3", 512 * j, 512 * j + 128), a("pA0", 128 * j, 128 * j + 128))
+        for j in range(3):
+            keep(a("t3", 512 * j + 128, 512 * j + 256), a("t3", 512 * j, 512 * j + 128), [[0, 128]], GE, 0.0, 0)
+            keep(a("t3", 512 * j + 256, 512 * j + 512), a("t3", 512 * j, 512 * j + 256), [[0, 256]], GE, 0.0, 0)
+        if v == 0:
+            iota(a("It", 1024, W), [[1, W - 1024]], -1024)
+
+        def c_list(lo, hi):
+            tt(a("z1", lo, hi), ind(a("uI"), a("l8", 0, (hi - lo) // 16)), a("krep", lo, hi), MUL)
+            if lo == 0:
+                ts(a("sI"), a("sq", 0, 8), 1.0 / 32, MUL, a("Acol"), ADD)
+            tt(a("zI", lo, hi), ind(a("sI"), a("l8", 0, (hi - lo) // 16)), a("z1", lo, hi), ADD)
+            ts(a("cX", 8 + lo, 8 + hi), a("zI", lo, hi), W - 1, AND)
+            cp(a("c16", lo, hi), a("cX", 8 + lo, 8 + hi))
+
+        def c_low(lo, hi):
+            cp(a("b16", lo, hi, half=1), a("cX", 8 + lo, 8 + hi, half=1))
+
+        c_list(0, 64)
+        if v == 0:
+            c_list(64, 256)
+            conv_q(2048, 3072, "S")
+            conv_q(3072, 3584, "V")
+            conv_q(3584, W, "S")
+
+        def q_sel(n):
+            lo, s = 512 * n, n // 2
+            tt(a("Qs", lo, lo + 512), ind(Qw, a("c16", lo // 16, lo // 16 + 32)), a("msk"), MUL)
+            if n % 2:
+                for r in range(16):
+                    mm(a(("pB", "pU")[s % 2], 0, 64), a("sel", 15 - r, 143 - r), a("Qs", 1024 * s + r, 1024 * s + 1024, 16),
+                       r == 0, r == 15)
+
+        def b_list(s):
+            pb = ("pB", "pU")[s % 2]
+            ts(a("c16", 64 * s, 64 * s + 64, half=1), a(pb, 0, 64, half=1), 2048.0 + W, ADD)
+            ts(a("b16", 64 * s, 64 * s + 64, half=0), a(pb, 0, 64, half=0), 2048.0 + W, ADD)
+
+        def x_ab(lo, n):
+            for t, lst in enumerate(("c16", "b16")):
+                act(a("AB", t * WB + 128 + lo, t * WB + 128 + lo + n), ind(a("X"), a(lst, lo // 16, (lo + n) // 16)))
+
+        items = [(c, j) for c, j in ITEMS]
+        ring = ("pA2", "pA0", "pA1", "pA3", "pD")
+
+        def span(c):
+            return (128 + 512 * c, 512) if c < 8 else (0, 128)
+
+        def line(n):
+            c, j = items[n]
+            lo, w = span(c)
+            bank, abs_ = ring[n % len(ring)], c in ON_SCALAR
+            ta, tb = a("AB", lo, lo + w), a("AB", WB + lo, WB + lo + w)
+            if abs_:
+                mm(a(bank, 0, w), idn[-1], a("t3", 512 * j, 512 * j + w), True, False)
+            if j < 2:
+                mm(a(bank, 0, w), a("Wl", 128 * j, 128 * j + 128), (ta, tb)[j], not abs_, True)
+            else:
+                mm(a(bank, 0, w, half=0), a("Wl", 256, 320), ta, not abs_, True)
+                mm(a(bank, 0, w, half=1), a("Wl", 320, 384), tb, not abs_, True)
+
+        def clip(n):
+            c, j = items[n]
+            lo, w = span(c)
+            dst, src = a("Mx", j * WB + lo, j * WB + lo + w), a(ring[n % len(ring)], 0, w)
+            if c in ON_SCALAR:
+                act(dst, src, ABS)
+            else:
+                tt(dst, src, a("t3", 512 * j, 512 * j + w), MIN if j == 2 else MAX)
+
+        def score(n):
+            c, j = items[n]
+            lo, w = span(c)
+            abs_ = c in ON_SCALAR
+            for m in range(lo, lo + w, 128):
+                o = a("pS", m // 128, 264, 33)
+                if abs_ and j == 0:
+                    mm(o, a("tsum"), a("bdh", 40, 48), False, False)
+                if not abs_ and j < 2:
+                    mm(o, a("AB", j * WB + m, j * WB + m + 128), (bdtop, bdbot)[j], False, False)
+                k = 8 * (j + 3 * abs_)
+                mm(o, a("Mx", j * WB + m, j * WB + m + 128), a("bdh", k, k + 8), False, False)
+
+        pl = a("off", 0, 8)
+        q_sel(0)
+        q_sel(1)
+        mm(a("pS", 0, 264), zrow, a("cg", 0, 264, rows=1), True, False)
+        for t in range(2):
+            act(a("AB", t * WB, t * WB + 128), a("pA0", 256 + 128 * t, 384 + 128 * t))
+        act(a("tsum"), a("pA1", 0, 128))
+        for c, bank in zip(y_front[v], ("pA3", "pD")):
+            y_out(c, bank)
+        c_low(0, 64)
+        cp(a("uP", 8, 16), a("pU", 0, 8))
+        if v:
+            c_list(64, 128)
+        b_list(0)
+        x_ab(0, 512)
+        x_ab(512, 512)
+        q_sel(2)
+        q_sel(3)
+        if v:
+            c_list(128, 256)
+        c_low(64, 256)
+        cp(a("Rf"), a(Rn))
+        b_list(1)
+        x_ab(1024, 1024)
+
+        def tables():
+            act(a("MLg"), ind(a("ML"), pl))
+            act(a("Tt", 128, 256), a("Rf"), scale=32.0)
+            mm(a("pB", 0, 272), r19, a("cg", rows=1), True, False)
+            mm(a("pU", 0, 16), r5, a("co", rows=1), True, False)
+
+        extra = {"T1": lambda: tt(a("T1"), ind(a("C1"), pl), a("Rf"), MUL),
+                 "q4": lambda: q_sel(4), "q5": lambda: q_sel(5), "q6": lambda: q_sel(6), "q7": lambda: q_sel(7),
+                 "b2": lambda: b_list(2), "b3": lambda: b_list(3),
+                 "x2": lambda: x_ab(2048, 1024), "x3": lambda: x_ab(3072, 1024), "tab": tables,
+                 "ct": lambda: tt(a("ctab"), ind(a("cX"), a("lc", 0, 17)), a("cm"), ADD),
+                 "M1": lambda: tt(a("M1"), ind(a("C3"), pl), a("Rf"), MUL),
+                 "Tt": lambda: tt(a("Tt", 0, 128), ind(a("C2"), pl), a("T1"), ADD),
+                 "MM": lambda: tt(a("MM"), ind(a("C4"), pl), a("M1"), ADD)}
+        for n in range(AHEAD):
+            line(n)
+        for n in range(len(items)):
+            clip(n)
+            for e in AFTER.get(n, ()):
+                extra[e]()
+            if n + AHEAD < len(items):
+                line(n + AHEAD)
+            score(n)
+        mm(a("pS", 0, 8), zrow, a("cu", 0, 8, rows=1), False, True)
+        scan(a("runE"), a("ce"), a("pS", 0, 264), 0.0, ADD, MIN)
+        ts(a("mP"), a("runE", 32, 264, 33), 6291488.0, ADD)
+        ts(a("mI"), a("mP"), 63, AND)
+        tt(a("lhM"), ind(a("mI"), a("lg")), a("diag"), MUL)
+        mm(a("pB", 0, 272), a("lhM"), a("eg"), False, True)
+        act(a("lhS"), a("lhM"), SIGN, acc=a("cnt"))
+        mm(a("pU", 0, 16), a("lhM"), a("eo", 0, 16), False, False)
+        mm(a("pU", 0, 16), a("lhS"), a("eo", 16, 32), False, True)
+        act(a("lf", 16, 24), a("pU", 8, 16), bias=r16)
+        act(a("lf", 8, 16), a("pU", 0, 8), bias=robias)
+        ts(a("n1"), a("uP"), 31, AND)
+        tt(a("n2"), a("n1"), a("nq"), ADD)
+        cp(a("n16"), a("n2"))
+        scan(a("runG"), a("pB", 0, 264), a("ctab", 0, 264), 0.0, MIN, MAX)
+        tt(a("lf", 0, 8), a("pB", 264, 272), a("runG", 32, 264, 33), ADD)
+        cp(a("l16"), a("lf"))
+        last = v + 1 == VISITS
+        for j, c in enumerate(y_back[v]):
+            y_x(c, "pA%d" % j)
+        if not last:
+            mm(a("pD", 0, 1), a("onf"), a("cnt"), True, True)
+            act(a("Acol"), a("pD", 0, 1), bias=-31.0 / 64)
+        for j, c in enumerate(y_back[v]):
+            y_q(c, "pA%d" % j)
+            y_out(c, "pA%d" % j)
+        cl = a("l16", 0, 8)
+        tt(a("h2"), ind(Qw, cl), a("MLg"), MUL)
+        tt(a("h1"), ind(Iw, cl), a("MM"), MUL)
+        tt(a("h3"), ind(a("Tt"), a("l16", 16, 24)), a("h2"), ADD)
+        tt(a("h4"), a("h1"), a("h3"), ADD)
+        ts(a("nI"), a("h4"), 5, SHR, W - 1, AND)
+        cp(a("S%d" % v), a("nI"))
+        sent += send(a("S%d" % v), "Rfin" if last else "R%d" % (v + 1), (rank - v if last else rank + 1) % n_ranks, v)
+        tt(a("ms"), ind(a("AB"), a("l16", 8, 16)), a("x5", 256, 384), ADD)
+        ts(a("nF"), a("nI"), 2048.0, SUB)
+        ts(a("mf"), a("ms"), 0.5, MUL, -0.25, ADD)
+        mb = a("mb", 0, 128)
+        cp(mb, a("mf"))
+        mm(a("pS", 0, 128), a("KQ"), a("nF"), True, False)
+        mm(a("pS", 0, 128), a("KX"), mb, False, True)
+        if not last:
+            for h in range(2):
+                mm(a("pS", 128, 256, half=h), a("idn", 64 - 64 * h, 128 - 64 * h), mb, True, True)
+            scatter(Xw, a("n16", 0, 8), mb)
+
+    act(a("Yn"), a("pS", 0, 128), bias=a("ybias"))
+    scatter(Yw, a("n16", 0, 8), a("Yn"))
+    dma("Y", T.yq[:, :], (T.Y[0:128:16, :], Yw[1]), "stQ", 1 << 17)
+    dma("S", T.yx[:, :], (T.Y[1:128:16, :], Yw[1]), "stX", 1 << 17)
+    arrive("Rfin", (rank + VISITS - 1) % n_ranks, VISITS - 1)
+    dma("Y", T.yr[:, :], a("Rfin"), "stR", 1 << 16)
+
+    def meet(x, y):
+        return any(p[0] == s[0] and (p[0] in _PS or (p[1] < s[2] and s[1] < p[2] and p[3] < s[4] and s[3] < p[4]))
+                   for p in x for s in y)
+
+    def psum(o):
+        return [r for r in o["r"] + o["w"] if r[0] in _PS]
+
+    def clash(e, o):
+        if e["q"] == o["q"] == "P":
+            return meet(e["w"], o["w"]) and not (e["adds"] and o["adds"])
+        return meet(e["w"], o["r"]) or meet(e["w"], o["w"]) or meet(e["r"], o["w"]) or (e["q"] != o["q"] and meet(psum(e), psum(o)))
+
+    if not _ORDER:
+        _ORDER.extend(plan(ops, clash))
+    ops = [ops[n] for n in _ORDER]
+    known = {q: {} for q in Q}
+    by_name = {}
+    for n, o in enumerate(ops):
+        o["waits"], o["need"] = [], False
+        own = o["sem"] is not None
+        o["key"] = o["sem"] if own else o["q"]
+        if len(_WAITS) == len(ops):
+            o["waits"] = _WAITS[n]
+            for m in o["waits"]:
+                ops[m]["need"] = True
+            continue
+        if o["q"] is not None:
+            names = {r[0] for r in o["r"] + o["w"]}
+            cand = sorted({m for nm in names for m in by_name.get(nm, [])}, reverse=True)
+            kn = known[o["q"]]
+            for m in cand:
+                e = ops[m]
+                if e["key"] == "remote" or kn.get(e["key"], -1) >= m:
+                    continue
+                dep = meet(e["w"], o["r"]) or meet(e["w"], o["w"]) or meet(e["r"], o["w"])
+                if e["key"] == o["q"] and not own:
+                    dep = dep and o["q"] != "P"
+                else:
+                    dep = dep or meet(psum(e), psum(o))
+                if dep:
+                    o["waits"].append(m)
+                    e["need"] = True
+                    kn[e["key"]] = m
+                    for kk, mm_ in e["clock"].items():
+                        kn[kk] = max(kn.get(kk, -1), mm_)
+            o["clock"] = dict(kn)
+        else:
+            o["clock"] = {}
+        for nm in {r[0] for r in o["r"] + o["w"]}:
+            by_name.setdefault(nm, []).append(n)
+    _WAITS[:] = [o["waits"] for o in ops]
+    count = {q: 0 for q in Q}
+    for o in ops:
+        if o["sem"] is None and o["need"]:
+            count[o["q"]] += 1
+            o["inc"], o["sem"], o["val"] = 1, "c" + o["q"], count[o["q"]]
+        else:
+            o["inc"] = 16 if (o["q"] is not None and o["sem"] not in (None, "remote")) else 0
+    for o in ops:
+        if o["q"] is None:
+            continue
+        for m in o["waits"]:
+            Q[o["q"]].wait_ge(T.sem[ops[m]["sem"]], ops[m]["val"])
+        ins = o["fn"]()
+        if o["inc"]:
+            ins.then_inc(T.sem[o["sem"]], o["inc"])
+    g.wait_ge(T.sem.sent, sent)
+    for s in ("stQ", "stX", "stR"):
+        g.wait_ge(T.sem[s], 16)

@@ -1,3 +1,4 @@
+import numpy as np
 from concourse.mybir import AluOpType, ActivationFunctionType
 
 ADD, SUB, MUL, MAX, MIN = AluOpType.add, AluOpType.subtract, AluOpType.mult, AluOpType.max, AluOpType.min
@@ -8,13 +9,18 @@ IDENT, ABS, SQUARE, SIGN = (ActivationFunctionType.Identity, ActivationFunctionT
 F32, BF, F16, I32, U16 = "float32", "bfloat16", "float16", "int32", "uint16"
 W, VISITS = 4096, 3
 SEND_ENGINES = 8
-ON_SCALAR = (3, 7)
-ITEMS = [(0, 0), (0, 1), (0, 2), (1, 0), (1, 1), (1, 2), (2, 0), (3, 0), (2, 1), (3, 1), (2, 2), (3, 2),
-         (4, 0), (4, 1), (4, 2), (5, 0), (5, 1), (5, 2), (6, 0), (7, 0), (6, 1), (7, 1), (6, 2), (7, 2), (8, 0), (8, 1), (8, 2)]
-AFTER = {1: ["q4"], 3: ["q5"], 5: ["b2", "x2"], 6: ["q6"], 8: ["q7"], 10: ["b3"], 11: ["x3", "tab"],
+ON_SCALAR = (7,)
+ITEMS = [(c, j) for c in (0, 8, 1, 2, 3, 4, 5) for j in range(3)] + [(c, j) for j in range(3) for c in (7, 6)]
+AFTER = {0: ["q4", "q5"], 1: ["b2", "x2"], 2: ["q6"], 3: ["q7"], 4: ["b3", "x3", "tab"],
          12: ["T1"], 13: ["ct"], 14: ["M1"], 15: ["Tt"], 16: ["MM"]}
 AHEAD = 3
-CYC, PE_CYC, GATHER, SCATTER, HANDOVER, DMA_RATE, PASSES = 1.04, 0.52, 1.5, 3.5, 80.0, 250.0, 8
+BANKS = [(1, 2, "S"), (3, 3, "S"), (6, 2, "S"), (8, 4, "V")]
+HALF0 = 1
+F6 = 2
+RING = ("pA0", "pA3", "pD", "pA1", "pA2")
+SEED, JITTER, SPREAD = 0, 0.15, ((1.04, 1500.0), (1.5, 2000.0), (2.08, 2500.0))
+B_ON_S, F1, F2, F3, F4, F5, HOP = (0, 1, 2, 3), 1, 0, 128, 1, 1, 1000.0
+CYC, PE_CYC, GATHER, SCATTER, HANDOVER, DMA_RATE, PASSES = 0.9, 0.45, 1.5, 3.5, 80.0, 300.0, 30
 
 _SB = {
     "X": (2 * W, BF), "Qi": (W, I32), "Qf": (W + 8, F32), "It": (W + 8, F32), "Y": (W, F32),
@@ -30,7 +36,7 @@ _SB = {
     "cu": (128, BF), "l11": (8, U16), "lg": (8, U16), "l8": (16, U16), "lc": (18, U16),
     "cm": (272, F32), "krep": (256, F32), "kh": (256, F16), "bdf": (128, F16),
     "OH": (16, BF), "ML": (16, F32), "C1": (16, F32), "C2": (16, F32), "C3": (16, F32), "C4": (16, F32),
-    "nq": (16, I32), "KQ": (128, F16), "KX": (128, BF), "q16": (1024, F16),
+    "nq": (16, I32), "KQ": (128, F16), "KX": (128, BF), "q16": (1536, F16),
     "x": (2048, BF), "ab": (1408, BF), "run1": (128, F32), "new": (128, F32), "sc3": (128, F32), "lhU": (128, F32),
     "uP": (16, I32), "uI": (8, I32), "sq": (16, F32), "sI": (8, I32), "z1": (256, F32), "zI": (256, I32),
     "cX": (264, I32), "c16": (256, U16), "off": (72, U16), "msk": (512, BF), "Qs": (W, F16), "b16": (256, U16),
@@ -38,7 +44,7 @@ _SB = {
     "ctab": (272, F32), "T1": (128, F32), "Tt": (256, F32), "M1": (128, F32), "MM": (128, F32), "MLg": (128, F32),
     "runE": (264, F32), "mP": (8, I32), "mI": (8, I32), "lhM": (128, BF), "lhS": (128, BF), "runG": (264, F32),
     "lf": (24, F32), "l16": (24, U16), "h1": (128, F32), "h2": (128, F32), "h3": (128, F32), "h4": (128, I32), "nI": (128, I32),
-    "n1": (16, I32), "n2": (16, I32), "n16": (16, U16), "ms": (128, F32), "mf": (128, I32), "mb": (256, BF),
+    "n1": (16, I32), "n2": (16, I32), "n16": (16, U16), "ms": (128, BF), "mf": (128, I32), "mb": (256, BF),
     "nF": (128, F16), "Yn": (128, F32),
 }
 _PS = ["pA0", "pA1", "pA2", "pA3", "pD", "pU", "pS", "pB"]
@@ -97,13 +103,31 @@ def plan(ops, clash):
             lo, hi = (mid + 1, hi) if spans[mid][1] <= t else (lo, mid)
         return lo
 
+    def issue(end):
+        return sorted(range(n_ops), key=lambda n: (end[n] - cost[n], end[n], n))
+
+    def span(order):
+        total = 0.0
+        for rate, hop in SPREAD:
+            free, end = {}, [0.0] * n_ops
+            for n in order:
+                t = max([end[m] + (lag if ops[n]["q"] else hop) for m, lag in pred[n]] + [free.get(unit[n], 0.0)])
+                free[unit[n]] = end[n] = t + plain[n] + ops[n]["picks"] * CYC * (rate - GATHER)
+            total += max(end) / (1.0 + 0.2 * rate)
+        return total
+
+    plain, rng = list(cost), np.random.default_rng(SEED)
     end = place(range(n_ops), pred)
-    best = end
-    for _ in range(PASSES):
-        back = place(sorted(range(n_ops), key=lambda n: (-end[n], -n)), succ)
+    best, least = end, None
+    for k in range(PASSES):
+        cost[:] = [c * f for c, f in zip(plain, (1.0 + JITTER * (k > 1) * rng.standard_normal(n_ops).clip(-2, 2)).tolist())]
+        back = place(sorted(range(n_ops), key=lambda n: (-best[n], -n)), succ)
+        cost[:] = plain
         end = place(sorted(range(n_ops), key=lambda n: (-back[n], n)), pred)
-        best = end if max(end) < max(best) else best
-    return last_dma + sorted(set(range(n_ops)) - set(last_dma), key=lambda n: (best[n] - cost[n], best[n], n))
+        length = span(issue(end))
+        if least is None or length < least:
+            best, least = end, length
+    return last_dma + [n for n in issue(best) if n not in last_dma]
 
 
 def rank_program(g, core, T, topo):
@@ -123,7 +147,10 @@ def rank_program(g, core, T, topo):
     def ind(win, off):
         return (win[0].indirect(off[0]), win[1] + off[1], 0, False)
 
+    picked = []
+
     def cost(out, x, rate=None):
+        picked.append(0 if x[2] else out[2])
         rate = GATHER if not x[2] else rate or (0.5 if out[3] and x[3] else 1.0)
         return 60.0 + out[2] * rate * CYC
 
@@ -135,7 +162,7 @@ def rank_program(g, core, T, topo):
 
     def op(q, fn, reads, writes, ns, sem=None, val=None, lat=0.0, nbytes=0, adds=False):
         ops.append({"q": q, "fn": fn, "r": reads, "w": writes, "sem": sem, "val": val, "cost": ns, "lat": lat,
-                    "bytes": nbytes, "adds": adds})
+                    "bytes": nbytes, "adds": adds, "picks": picked.pop() if picked else 0})
 
     def ts(out, x, s1, o0, s2=None, o1=None):
         if o1 is None:
@@ -186,7 +213,7 @@ def rank_program(g, core, T, topo):
         engs = topo.engines(core, to)[:SEND_ENGINES]
         m = sum(1 << e for e in engs)
         op("G", lambda: g.remote_dma(T[dst_name][:, :], src[0], T.sem["arr%d" % v], T.sem.sent, pid, rid, m), rg(src), [],
-           300.0, "remote", 0, 2500.0)
+           300.0, "remote", 0, HOP)
         return len(engs)
 
     def arrive(name, from_rank, v):
@@ -200,7 +227,7 @@ def rank_program(g, core, T, topo):
     dma("S", a("X", 2048, W), T.xf[:, 2048:W], "ldX1", 1 << 19)
     for j in range(4):
         dma("Y", a("Qi", 1024 * j, 1024 * j + 1024), T.pa[:, 1024 * j:1024 * j + 1024], "ldQ%d" % j, 1 << 19)
-    for h in range(2):
+    for h in range(0 if F6 else 2):
         dma("Y", a("X", W, 2 * W, half=h), T.xf[64 - 64 * h:128 - 64 * h, :], "ldX%d" % (2 + h), 1 << 19)
 
     r16, g16 = a("r16"), a("g16")
@@ -320,9 +347,9 @@ def rank_program(g, core, T, topo):
 
     Xw, Qw, Iw, Yw = a("X", 0, W), a("Qf"), a("It"), a("Y")
     WB = W + 128
-    banks = [(1, 3, "V"), (4, 3, "S"), (7, 2, "V"), (9, 3, "S")]
-    y_front = [[], [2, 3], [6, 7]]
-    y_back = [[0, 1], [4, 5], []]
+    banks = BANKS
+    y_back = [[0, 1, 2], [3, 4, 5], [6, 7]]
+    y_bank = ("pA0", "pA1", "pA3")
     sent = 0
 
     def conv_q(lo, hi, q):
@@ -335,7 +362,7 @@ def rank_program(g, core, T, topo):
         mm(a(bank), a("KX"), a("X", 512 * c, 512 * c + 512), True, False)
 
     def y_q(c, bank):
-        q16 = a("q16", 512 * (c % 2), 512 * (c % 2) + 512)
+        q16 = a("q16", 512 * (c % 3), 512 * (c % 3) + 512)
         act(q16, a("Qf", 512 * c, 512 * c + 512))
         mm(a(bank), a("KQ"), q16, False, True)
 
@@ -352,7 +379,7 @@ def rank_program(g, core, T, topo):
             cp(a("x", 1024 * h, 1024 * h + 512), ind(Xw, a(Rn, 64 * h, 64 * h + 32)))
             act(a("x", 1024 * h + 512, 1024 * h + 1024), ind(Xw, a(Rn, 64 * h + 32, 64 * h + 64)))
             for b, (k0, nk, who) in enumerate(banks):
-                for j in range(nk):
+                for j in range(nk if who == "S" else 0):
                     o = a("pA%d" % b, 128 * j + 64 * h, 128 * j + 64 * h + 64)
                     mm(o, idn[1], a("x", 1024 * h + k0 + j + 1, 1024 * h + 1024, 16), True, False)
                     mm(o, idn[-1], a("x", 1024 * h + k0 + j, 1024 * h + 1024, 16), False, True)
@@ -367,11 +394,12 @@ def rank_program(g, core, T, topo):
             for k in range(k0, k0 + nk):
                 if who == "V":
                     mm(a("pD", k, 128, 16), a("x", k + 1, 2048, 16), bdm1, False, False)
-                    mm(a("pD", k, 128, 16), a("x", k, 2048, 16), bd1, False, False)
+                    mm(a("pD", k, 128, 16), a("x", k, 2048, 16), bdm1, False, False)
         for b, (k0, nk, who) in enumerate(banks):
             dst, src = a("ab", 128 * (k0 - 1), 128 * (k0 - 1 + nk)), a("pA%d" % b, 0, 128 * nk)
             if who == "V":
-                ts(dst, src, 0.0, MAX)
+                for k in range(k0, k0 + nk):
+                    tt(a("ab", 128 * (k - 1), 128 * k), a("x", k + 1, 2048, 16), a("x", k, 2048, 16), MAX)
             else:
                 act(dst, src, ABS)
             for k in range(k0, k0 + nk):
@@ -381,6 +409,11 @@ def rank_program(g, core, T, topo):
         mm(a("pD", 0, 8), zrow, a("cu", 0, 8, rows=1), False, True)
         mm(a("pU", 0, 8), zrow, a("cu", 0, 8, rows=1), False, True)
         if v == 0:
+            for c in range(8 if F6 else 0):
+                bank = ("pS", "pA3")[c % 2]
+                for h in range(2):
+                    mm(a(bank, half=h), a("idn", 64 - 64 * h, 128 - 64 * h), a("X", 512 * c, 512 * c + 512), True, True)
+                (act if c % F6 else cp)(a("X", W + 512 * c, W + 512 * c + 512), a(bank))
             conv_q(0, 1024, "S")
             conv_q(1024, 2048, "S")
         if v:
@@ -397,32 +430,29 @@ def rank_program(g, core, T, topo):
         if v:
             scatter(Yw, a("n16", 0, 8), a("Yn"))
         cp(a("uP", 0, 8), a("pB", 0, 8))
-        ts(a("off"), a("pD", 0, 72), -0.4961, ADD)
+        if F5:
+            act(a("off"), a("pD", 0, 72), bias=-0.4961)
+        else:
+            ts(a("off"), a("pD", 0, 72), -0.4961, ADD)
         ts(a("uI"), a("uP", 0, 8), W - 1, AND)
         act(a("sq"), ind(a("uI"), a("l8", 0, 1)), SQUARE, bias=-2048.0)
         act(a("msk"), ind(a("OH"), a("off", 0, 32)))
         act(a("x5"), ind(a("x"), a("off", 32, 72)))
-        if y_front[v]:
-            y_x(y_front[v][0], "pA3")
-            y_q(y_front[v][0], "pA3")
-        for j, (f, s) in enumerate(((2, 3), (1, 0))):
-            xf_, xs_ = a("x5", 128 * f, 128 * f + 128), a("x5", 128 * s, 128 * s + 128)
-            lo, up = a("idn", 0, 64), a("idn", 64, 128)
-            mm(a("pA0", 256 * j, 256 * j + 128, half=0), lo, xf_, True, True)
-            mm(a("pA0", 256 * j, 256 * j + 128, half=1), lo, xs_, True, True)
-            mm(a("pA0", 256 * j + 128, 256 * j + 256, half=0), up, xs_, True, True)
-            mm(a("pA0", 256 * j + 128, 256 * j + 256, half=1), up, xf_, True, True)
-        for j, c in enumerate((1, 1, -1)):
-            mm(a("pA1", 0, 128), idn[c], a("x5", 256 + 128 * j, 384 + 128 * j), j == 0, j == 2)
-        if y_front[v]:
-            y_x(y_front[v][1], "pD")
-            y_q(y_front[v][1], "pD")
+
+        def pairs():
+            for j, (f, s) in enumerate(((2, 3), (1, 0))):
+                xf_, xs_ = a("x5", 128 * f, 128 * f + 128), a("x5", 128 * s, 128 * s + 128)
+                lo, up = a("idn", 0, 64), a("idn", 64, 128)
+                for t, (w, first, second) in enumerate(((lo, xf_, xs_), (up, xs_, xf_))):
+                    bank, c = ("pA1", "pA2")[j], 128 * t
+                    mm(a(bank, c, c + 128, half=0), w, first, True, True)
+                    mm(a(bank, c, c + 128, half=1), w, second, True, True)
+            for j, c in enumerate((1, 1, -1)):
+                mm(a("pA2", 256, 384), idn[c], a("x5", 256 + 128 * j, 384 + 128 * j), j == 0, j == 2)
+
         keep(a("t3", 1024, 1152), a("x5", 512, 640), [[0, 128]], GE, 0.0, 0)
-        for j in range(2):
-            act(a("t3", 512 * j, 512 * j + 128), a("pA0", 128 * j, 128 * j + 128))
-        for j in range(3):
-            keep(a("t3", 512 * j + 128, 512 * j + 256), a("t3", 512 * j, 512 * j + 128), [[0, 128]], GE, 0.0, 0)
-            keep(a("t3", 512 * j + 256, 512 * j + 512), a("t3", 512 * j, 512 * j + 256), [[0, 256]], GE, 0.0, 0)
+        keep(a("t3", 1152, 1280), a("x5", 512, 640), [[0, 128]], GE, 0.0, 0)
+        keep(a("t3", 1280, 1536), a("t3", 1024, 1280), [[0, 256]], GE, 0.0, 0)
         if v == 0:
             iota(a("It", 1024, W), [[1, W - 1024]], -1024)
 
@@ -432,10 +462,10 @@ def rank_program(g, core, T, topo):
                 ts(a("sI"), a("sq", 0, 8), 1.0 / 32, MUL, a("Acol"), ADD)
             tt(a("zI", lo, hi), ind(a("sI"), a("l8", 0, (hi - lo) // 16)), a("z1", lo, hi), ADD)
             ts(a("cX", 8 + lo, 8 + hi), a("zI", lo, hi), W - 1, AND)
-            cp(a("c16", lo, hi), a("cX", 8 + lo, 8 + hi))
+            (act if F2 and lo else cp)(a("c16", lo, hi), a("cX", 8 + lo, 8 + hi))
 
         def c_low(lo, hi):
-            cp(a("b16", lo, hi, half=1), a("cX", 8 + lo, 8 + hi, half=1))
+            (act if F1 else cp)(a("b16", lo, hi, half=1), a("cX", 8 + lo, 8 + hi, half=1))
 
         c_list(0, 64)
         if v == 0:
@@ -447,22 +477,33 @@ def rank_program(g, core, T, topo):
         def q_sel(n):
             lo, s = 512 * n, n // 2
             tt(a("Qs", lo, lo + 512), ind(Qw, a("c16", lo // 16, lo // 16 + 32)), a("msk"), MUL)
-            if n % 2:
+            if HALF0 and n < 2:
+                for r in range(16):
+                    mm(a(("pB", "pS")[n], 0, 32), a("sel", 15 - r, 143 - r), a("Qs", lo + r, lo + 512, 16), r == 0, r == 15)
+                act(a("c16", 32 * n, 32 * n + 32, half=1), a(("pB", "pS")[n], 0, 32, half=1), bias=2048.0 + W)
+                act(a("b16", 32 * n, 32 * n + 32, half=0), a(("pB", "pS")[n], 0, 32, half=0), bias=2048.0 + W)
+            elif n % 2:
                 for r in range(16):
                     mm(a(("pB", "pU")[s % 2], 0, 64), a("sel", 15 - r, 143 - r), a("Qs", 1024 * s + r, 1024 * s + 1024, 16),
                        r == 0, r == 15)
 
         def b_list(s):
             pb = ("pB", "pU")[s % 2]
-            ts(a("c16", 64 * s, 64 * s + 64, half=1), a(pb, 0, 64, half=1), 2048.0 + W, ADD)
-            ts(a("b16", 64 * s, 64 * s + 64, half=0), a(pb, 0, 64, half=0), 2048.0 + W, ADD)
+            if HALF0 and s == 0:
+                pass
+            elif s in B_ON_S:
+                act(a("c16", 64 * s, 64 * s + 64, half=1), a(pb, 0, 64, half=1), bias=2048.0 + W)
+                act(a("b16", 64 * s, 64 * s + 64, half=0), a(pb, 0, 64, half=0), bias=2048.0 + W)
+            else:
+                ts(a("c16", 64 * s, 64 * s + 64, half=1), a(pb, 0, 64, half=1), 2048.0 + W, ADD)
+                ts(a("b16", 64 * s, 64 * s + 64, half=0), a(pb, 0, 64, half=0), 2048.0 + W, ADD)
 
         def x_ab(lo, n):
             for t, lst in enumerate(("c16", "b16")):
                 act(a("AB", t * WB + 128 + lo, t * WB + 128 + lo + n), ind(a("X"), a(lst, lo // 16, (lo + n) // 16)))
 
         items = [(c, j) for c, j in ITEMS]
-        ring = ("pA2", "pA0", "pA1", "pA3", "pD")
+        ring = RING
 
         def span(c):
             return (128 + 512 * c, 512) if c < 8 else (0, 128)
@@ -503,27 +544,29 @@ def rank_program(g, core, T, topo):
                 mm(o, a("Mx", j * WB + m, j * WB + m + 128), a("bdh", k, k + 8), False, False)
 
         pl = a("off", 0, 8)
+        c_low(0, 64)
         q_sel(0)
+        pairs()
+        for t in range(2):
+            act(a("t3", 512 * t, 512 * t + 128), a("pA1", 128 * t, 128 * t + 128))
+            keep(a("t3", 512 * t + 128, 512 * t + 256), a("t3", 512 * t, 512 * t + 128), [[0, 128]], GE, 0.0, 0)
+            keep(a("t3", 512 * t + 256, 512 * t + 512), a("t3", 512 * t, 512 * t + 256), [[0, 256]], GE, 0.0, 0)
+        x_ab(0, 512)
         q_sel(1)
+        x_ab(512, 512)
         mm(a("pS", 0, 264), zrow, a("cg", 0, 264, rows=1), True, False)
         for t in range(2):
-            act(a("AB", t * WB, t * WB + 128), a("pA0", 256 + 128 * t, 384 + 128 * t))
-        act(a("tsum"), a("pA1", 0, 128))
-        for c, bank in zip(y_front[v], ("pA3", "pD")):
-            y_out(c, bank)
-        c_low(0, 64)
-        cp(a("uP", 8, 16), a("pU", 0, 8))
+            act(a("AB", t * WB, t * WB + 128), a("pA2", 128 * t, 128 + 128 * t))
+        act(a("tsum"), a("pA2", 256, 384))
+        (act if F4 else cp)(a("uP", 8, 16), a("pU", 0, 8))
         if v:
-            c_list(64, 128)
-        b_list(0)
-        x_ab(0, 512)
-        x_ab(512, 512)
+            c_list(64, F3)
         q_sel(2)
         q_sel(3)
-        if v:
-            c_list(128, 256)
+        if v and F3 < 256:
+            c_list(F3, 256)
         c_low(64, 256)
-        cp(a("Rf"), a(Rn))
+        (act if F4 else cp)(a("Rf"), a(Rn))
         b_list(1)
         x_ab(1024, 1024)
 
@@ -559,23 +602,29 @@ def rank_program(g, core, T, topo):
         act(a("lhS"), a("lhM"), SIGN, acc=a("cnt"))
         mm(a("pU", 0, 16), a("lhM"), a("eo", 0, 16), False, False)
         mm(a("pU", 0, 16), a("lhS"), a("eo", 16, 32), False, True)
-        act(a("lf", 16, 24), a("pU", 8, 16), bias=r16)
-        act(a("lf", 8, 16), a("pU", 0, 8), bias=robias)
+        act(a("l16", 16, 24), a("pU", 8, 16), bias=r16)
+        act(a("l16", 8, 16), a("pU", 0, 8), bias=robias)
+        mb = a("mb", 0, 128)
+        act(a("ms"), ind(a("AB"), a("l16", 8, 16)))
+        mm(a("pA2", 0, 128), idn[1], a("x5", 256, 384), True, False)
+        mm(a("pA2", 0, 128), idn[1], a("ms"), False, True)
+        act(a("mf"), a("pA2", 0, 128), bias=-0.25, scale=0.5)
+        act(mb, a("mf"))
         ts(a("n1"), a("uP"), 31, AND)
         tt(a("n2"), a("n1"), a("nq"), ADD)
         cp(a("n16"), a("n2"))
         scan(a("runG"), a("pB", 0, 264), a("ctab", 0, 264), 0.0, MIN, MAX)
         tt(a("lf", 0, 8), a("pB", 264, 272), a("runG", 32, 264, 33), ADD)
-        cp(a("l16"), a("lf"))
+        cp(a("l16", 0, 8), a("lf", 0, 8))
         last = v + 1 == VISITS
         for j, c in enumerate(y_back[v]):
-            y_x(c, "pA%d" % j)
+            y_x(c, y_bank[j])
         if not last:
             mm(a("pD", 0, 1), a("onf"), a("cnt"), True, True)
             act(a("Acol"), a("pD", 0, 1), bias=-31.0 / 64)
         for j, c in enumerate(y_back[v]):
-            y_q(c, "pA%d" % j)
-            y_out(c, "pA%d" % j)
+            y_q(c, y_bank[j])
+            y_out(c, y_bank[j])
         cl = a("l16", 0, 8)
         tt(a("h2"), ind(Qw, cl), a("MLg"), MUL)
         tt(a("h1"), ind(Iw, cl), a("MM"), MUL)
@@ -584,11 +633,7 @@ def rank_program(g, core, T, topo):
         ts(a("nI"), a("h4"), 5, SHR, W - 1, AND)
         cp(a("S%d" % v), a("nI"))
         sent += send(a("S%d" % v), "Rfin" if last else "R%d" % (v + 1), (rank - v if last else rank + 1) % n_ranks, v)
-        tt(a("ms"), ind(a("AB"), a("l16", 8, 16)), a("x5", 256, 384), ADD)
-        ts(a("nF"), a("nI"), 2048.0, SUB)
-        ts(a("mf"), a("ms"), 0.5, MUL, -0.25, ADD)
-        mb = a("mb", 0, 128)
-        cp(mb, a("mf"))
+        act(a("nF"), a("nI"), bias=-2048.0)
         mm(a("pS", 0, 128), a("KQ"), a("nF"), True, False)
         mm(a("pS", 0, 128), a("KX"), mb, False, True)
         if not last:

import numpy as np
from concourse.mybir import AluOpType, ActivationFunctionType

ADD, SUB, MUL, MAX, MIN = AluOpType.add, AluOpType.subtract, AluOpType.mult, AluOpType.max, AluOpType.min
EQ, NE, GT, GE, LT = AluOpType.is_equal, AluOpType.not_equal, AluOpType.is_gt, AluOpType.is_ge, AluOpType.is_lt
AND, SHR = AluOpType.bitwise_and, AluOpType.arith_shift_right
IDENT, ABS, SQUARE, SIGN = (ActivationFunctionType.Identity, ActivationFunctionType.Abs,
                            ActivationFunctionType.Square, ActivationFunctionType.Sign)
F32, BF, F16, I32, U16 = "float32", "bfloat16", "float16", "int32", "uint16"
W, VISITS = 4096, 3
SEND_ENGINES = 8
ON_SCALAR = (7,)
ITEMS = [(c, j) for c in (0, 8, 1, 2, 3, 4, 5) for j in range(3)] + [(c, j) for j in range(3) for c in (7, 6)]
AFTER = {0: ["q4", "q5"], 1: ["b2", "x2"], 2: ["q6"], 3: ["q7"], 4: ["b3", "x3", "tab"],
         12: ["T1"], 13: ["ct"], 14: ["M1"], 15: ["Tt"], 16: ["MM"]}
AHEAD = 3
BANKS = [(1, 2, "S"), (3, 3, "S"), (6, 2, "S"), (8, 4, "V")]
HALF0 = 1
F6 = 2
RING = ("pA0", "pA3", "pD", "pA1", "pA2")
SEED, JITTER, SPREAD = 0, 0.15, ((1.04, 1500.0), (1.5, 2000.0), (2.08, 2500.0))
B_ON_S, F1, F2, F3, F4, F5, HOP = (0, 1, 2, 3), 1, 0, 128, 1, 1, 1000.0
CYC, PE_CYC, GATHER, SCATTER, HANDOVER, DMA_RATE, PASSES = 0.9, 0.45, 1.5, 3.5, 80.0, 300.0, 30

_SB = {
    "X": (2 * W, BF), "Qi": (W, I32), "Qf": (W + 8, F32), "It": (W + 8, F32), "Y": (W, F32),
    "Ri": (128, I32), "wI": (4, I32), "kI": (4, I32), "wF": (1, F32), "kF": (2, F32),
    "R0": (128, U16), "R1": (128, U16), "R2": (128, U16), "Rfin": (128, F32),
    "S0": (128, U16), "S1": (128, U16), "S2": (128, F32), "Rf": (128, F32),
    "pI": (16, I32), "pJ": (16, I32), "r16": (1, F32), "g16": (1, F32), "cols": (32, F32),
    "ybias": (1, F32), "Acol": (1, F32), "cnt": (1, F32),
    "tM": (144, BF), "tB": (72, BF), "tA": (520, BF), "tD": (16, F32), "tE": (128, F32), "tI": (48, I32), "tJ": (32, I32),
    "sel": (144, F16), "idn": (256, BF), "Wl": (384, BF), "bdb": (48, BF), "bdh": (48, F16), "diag": (128, BF),
    "eu": (8, F32), "ep": (72, F32), "cp": (72, F16), "lhc": (128, F16), "rowc": (384, BF), "onf": (128, F32),
    "eg": (272, BF), "cg": (272, BF), "eo": (32, BF), "co": (16, BF), "c1": (128, F32), "ce": (264, F32),
    "cu": (128, BF), "l11": (8, U16), "lg": (8, U16), "l8": (16, U16), "lc": (18, U16),
    "cm": (272, F32), "krep": (256, F32), "kh": (256, F16), "bdf": (128, F16),
    "OH": (16, BF), "ML": (16, F32), "C1": (16, F32), "C2": (16, F32), "C3": (16, F32), "C4": (16, F32),
    "nq": (16, I32), "KQ": (128, F16), "KX": (128, BF), "q16": (1536, F16),
    "x": (2048, BF), "ab": (1408, BF), "run1": (128, F32), "new": (128, F32), "sc3": (128, F32), "lhU": (128, F32),
    "uP": (16, I32), "uI": (8, I32), "sq": (16, F32), "sI": (8, I32), "z1": (256, F32), "zI": (256, I32),
    "cX": (264, I32), "c16": (256, U16), "off": (72, U16), "msk": (512, BF), "Qs": (W, F16), "b16": (256, U16),
    "AB": (2 * (W + 128), BF), "x5": (640, BF), "tsum": (128, F16), "t3": (1536, BF), "Mx": (3 * (W + 128), F16),
    "ctab": (272, F32), "T1": (128, F32), "Tt": (256, F32), "M1": (128, F32), "MM": (128, F32), "MLg": (128, F32),
    "runE": (264, F32), "mP": (8, I32), "mI": (8, I32), "lhM": (128, BF), "lhS": (128, BF), "runG": (264, F32),
    "lf": (24, F32), "l16": (24, U16), "h1": (128, F32), "h2": (128, F32), "h3": (128, F32), "h4": (128, I32), "nI": (128, I32),
    "n1": (16, I32), "n2": (16, I32), "n16": (16, U16), "ms": (128, BF), "mf": (128, I32), "mb": (256, BF),
    "nF": (128, F16), "Yn": (128, F32),
}
_PS = ["pA0", "pA1", "pA2", "pA3", "pD", "pU", "pS", "pB"]
SCRATCH = {k: ("sbuf", [128, v[0]], v[1]) for k, v in _SB.items()}
SCRATCH.update({k: ("psum", [128, 512], F32) for k in _PS})
SEMAPHORES = ["cV", "cS", "cP", "cG", "ldR", "ldW", "ldK", "ldX0", "ldX1", "ldX2", "ldX3", "ldQ0", "ldQ1", "ldQ2", "ldQ3",
              "arr0", "arr1", "arr2", "sent", "stR", "stQ", "stX"]


_ORDER, _WAITS = [], []


def plan(ops, clash):
    n_ops = len(ops)
    pred, succ, seen, sends = [set() for _ in ops], [[] for _ in ops], {}, []
    last_dma = []
    for n, o in enumerate(ops):
        names = {r[0] for r in o["r"] + o["w"]}
        for m in {m for nm in names for m in seen.get(nm, [])}:
            if clash(ops[m], o):
                pred[n].add(m)
        if o["q"] is None:
            pred[n].add(sends[-1])
        if o["sem"] == "remote":
            sends.append(n)
        elif o["bytes"] and not o["r"]:
            pred[n].update(last_dma[-1:])
            last_dma.append(n)
        for nm in names:
            seen.setdefault(nm, []).append(n)
    unit = ["D" if o["bytes"] else o["q"] for o in ops]
    cost = [o["bytes"] / DMA_RATE if o["bytes"] else o["cost"] for o in ops]
    pred = [[(m, 0.0 if unit[m] == unit[n] and unit[n] in "PD" else ops[m]["lat"] + HANDOVER) for m in p] if ops[n]["q"] else
            [(m, ops[m]["lat"]) for m in p] for n, p in enumerate(pred)]
    for n, p in enumerate(pred):
        for m, lag in p:
            succ[m].append((n, lag))

    def place(order, before):
        busy, end = {}, [0.0] * n_ops
        for n in order:
            t = max([end[m] + lag for m, lag in before[n]] + [0.0])
            spans = busy.setdefault(unit[n], [])
            k = bisect(spans, t)
            while k < len(spans) and spans[k][0] < t + cost[n]:
                t = max(t, spans[k][1])
                k += 1
            spans.insert(k, (t, t + cost[n]))
            end[n] = t + cost[n]
        return end

    def bisect(spans, t):
        lo, hi = 0, len(spans)
        while lo < hi:
            mid = (lo + hi) // 2
            lo, hi = (mid + 1, hi) if spans[mid][1] <= t else (lo, mid)
        return lo

    def issue(end):
        return sorted(range(n_ops), key=lambda n: (end[n] - cost[n], end[n], n))

    def span(order):
        total = 0.0
        for rate, hop in SPREAD:
            free, end = {}, [0.0] * n_ops
            for n in order:
                t = max([end[m] + (lag if ops[n]["q"] else hop) for m, lag in pred[n]] + [free.get(unit[n], 0.0)])
                free[unit[n]] = end[n] = t + plain[n] + ops[n]["picks"] * CYC * (rate - GATHER)
            total += max(end) / (1.0 + 0.2 * rate)
        return total

    plain, rng = list(cost), np.random.default_rng(SEED)
    end = place(range(n_ops), pred)
    best, least = end, None
    for k in range(PASSES):
        cost[:] = [c * f for c, f in zip(plain, (1.0 + JITTER * (k > 1) * rng.standard_normal(n_ops).clip(-2, 2)).tolist())]
        back = place(sorted(range(n_ops), key=lambda n: (-best[n], -n)), succ)
        cost[:] = plain
        end = place(sorted(range(n_ops), key=lambda n: (-back[n], n)), pred)
        length = span(issue(end))
        if least is None or length < least:
            best, least = end, length
    return last_dma + [n for n in issue(best) if n not in last_dma]


def rank_program(g, core, T, topo):
    rank = T.rank_of(core)
    if rank is None:
        return
    n_ranks = len(T.cores)
    Q = {"V": g.vector, "S": g.scalar, "P": g.tensor, "G": g, "Y": g.sync}
    ops = []

    def a(name, lo=0, hi=None, st=1, rows=128, half=None):
        hi = SCRATCH[name][1][1] if hi is None else hi
        cols = slice(lo, hi) if st == 1 else slice(lo, hi, st)
        p0, p1 = (0, rows) if half is None else (64 * half, 64 * half + 64)
        return (T[name][p0:p1, cols], [(name, lo, hi, p0, p1)], len(range(lo, hi, st)), SCRATCH[name][2] in (BF, F16, U16))

    def ind(win, off):
        return (win[0].indirect(off[0]), win[1] + off[1], 0, False)

    picked = []

    def cost(out, x, rate=None):
        picked.append(0 if x[2] else out[2])
        rate = GATHER if not x[2] else rate or (0.5 if out[3] and x[3] else 1.0)
        return 60.0 + out[2] * rate * CYC

    def ap(x):
        return x[0] if isinstance(x, tuple) else x

    def rg(*xs):
        return [r for x in xs if isinstance(x, tuple) for r in x[1]]

    def op(q, fn, reads, writes, ns, sem=None, val=None, lat=0.0, nbytes=0, adds=False):
        ops.append({"q": q, "fn": fn, "r": reads, "w": writes, "sem": sem, "val": val, "cost": ns, "lat": lat,
                    "bytes": nbytes, "adds": adds, "picks": picked.pop() if picked else 0})

    def ts(out, x, s1, o0, s2=None, o1=None):
        if o1 is None:
            op("V", lambda: g.vector.tensor_scalar(out[0], x[0], ap(s1), None, o0), rg(x, s1), rg(out), cost(out, x))
        else:
            op("V", lambda: g.vector.tensor_scalar(out[0], x[0], ap(s1), ap(s2), o0, o1), rg(x, s1, s2), rg(out), cost(out, x))

    def tt(out, x, y, o):
        op("V", lambda: g.vector.tensor_tensor(out[0], x[0], y[0], o), rg(x, y), rg(out),
           cost(out, x, 1.0 if x[1][0][0] in _PS else 2.0))

    def cp(out, x):
        op("V", lambda: g.vector.tensor_copy(out[0], x[0]), rg(x), rg(out), cost(out, x))

    def scatter(win, off, x):
        op("V", lambda: g.vector.tensor_copy(win[0].indirect(off[0]), x[0]), rg(x, off), rg(win), cost(x, x, SCATTER))

    def scan(out, d0, d1, init, o0, o1):
        op("V", lambda: g.vector.tensor_tensor_scan(out[0], d0[0], d1[0], init, o0, o1), rg(d0, d1), rg(out), cost(out, d0))

    def fill(out, c):
        op("V", lambda: g.vector.memset(out[0], c), [], rg(out), cost(out, out))

    def act(out, x, f=IDENT, bias=0.0, scale=1.0, acc=None):
        op("S", lambda: g.scalar.activation(out[0], x[0], f, bias=ap(bias), scale=scale, accum_out=ap(acc)),
           rg(x, bias), rg(out, acc), 10.0 + cost(out, x, 1.0))

    def mm(out, l, r, start, stop):
        op("P", lambda: g.tensor.matmul(out[0], l[0], r[0], start, stop), rg(l, r), rg(out),
           10.0 + max(min(64, l[2]), r[2]) * PE_CYC * (1 if l[3] else 4), lat=60.0, adds=not (start or stop))

    def iota(out, pat, base=0, cmul=0):
        if SCRATCH[out[1][0][0]][2] == I32:
            op("G", lambda: g.iota(out[0], pat, base, cmul), [], rg(out), 70.0 + cost(out, out, 2.0))
        else:
            op("G", lambda: g.iota(out[0], pat, base, cmul, allow_small_or_imprecise_dtypes=True), [], rg(out),
               70.0 + cost(out, out, 2.0))

    def keep(out, x, pat, cmp_, other, base):
        op("G", lambda: g.affine_select(out[0], x[0], pat, cmp_, other, base, 0), rg(x), rg(out), 110.0 + cost(out, out, 2.0))

    def dma(q, out, x, sem, nbytes):
        op(q, lambda: Q[q].dma_start(ap(out), ap(x)), rg(x), rg(out), 100.0, sem, 16, 1800.0, nbytes)

    def send(src, dst_name, to_rank, v):
        to = T.cores[to_rank]
        rid, pid, _ = topo.addr(to)
        engs = topo.engines(core, to)[:SEND_ENGINES]
        m = sum(1 << e for e in engs)
        op("G", lambda: g.remote_dma(T[dst_name][:, :], src[0], T.sem["arr%d" % v], T.sem.sent, pid, rid, m), rg(src), [],
           300.0, "remote", 0, HOP)
        return len(engs)

    def arrive(name, from_rank, v):
        n = len(topo.engines(T.cores[from_rank], core)[:SEND_ENGINES])
        op(None, None, [], rg(a(name)), 0.0, "arr%d" % v, n)

    dma("S", a("Ri"), T.rp[:, :], "ldR", 65536)
    dma("Y", a("wI", 0, 1), T.wt[:, :], "ldW", 512)
    dma("S", a("kI", 0, 2), T.kap[:, :], "ldK", 1024)
    dma("Y", a("X", 0, 2048), T.xf[:, 0:2048], "ldX0", 1 << 19)
    dma("S", a("X", 2048, W), T.xf[:, 2048:W], "ldX1", 1 << 19)
    for j in range(4):
        dma("Y", a("Qi", 1024 * j, 1024 * j + 1024), T.pa[:, 1024 * j:1024 * j + 1024], "ldQ%d" % j, 1 << 19)
    for h in range(0 if F6 else 2):
        dma("Y", a("X", W, 2 * W, half=h), T.xf[64 - 64 * h:128 - 64 * h, :], "ldX%d" % (2 + h), 1 << 19)

    r16, g16 = a("r16"), a("g16")
    pcol, npcol, p16, kgt, r1, g17, hi, sgn, p64, g64, g64b, gsw, top64, bot64, robias = (a("cols", j, j + 1) for j in range(15))
    col, blk8 = a("tM", 15, 143), a("tB", 0, 8)
    zrow, r5, r19 = (a("rowc", 128 * j, 128 * j + 128, rows=1) for j in range(3))
    iota(a("pI"), [[0, 16]], 0, 1)
    iota(a("tM"), [[1, 144]], -15)
    iota(a("tB"), [[0, 9], [16, 8]])
    iota(a("cu"), [[0, 8], [1, 16]])
    iota(a("tI", 0, 8), [[16, 8]], 11)
    iota(a("tI", 8, 16), [[1, 8]])
    iota(a("tE", 0, 40), [[1, 5], [256, 8]], -1)
    iota(a("tA", 0, 128), [[16, 8], [0, 16]])
    iota(a("tA", 128, 256), [[1, 16], [0, 8]])
    fill(a("c1"), 1.0e6)
    fill(a("rowc", 0, 128), 0.0)
    fill(a("rowc", 128, 256), 2.0 ** -5)
    fill(a("rowc", 256, 384), 2.0 ** 19)
    keep(a("c1"), a("c1"), [[0, 8], [1, 16]], GE, -1.0, -1)
    keep(a("c1"), a("c1"), [[0, 8], [-1, 16]], GE, -1.0, 11)
    iota(a("tA", 256, 520), [[16, 8], [0, 33]])
    iota(a("tI", 16, 33), [[16, 17]])
    iota(a("cg", 0, 264), [[0, 8], [2, 33]], -1)
    iota(a("cg", 264, 272), [[0, 8]])
    fill(a("new", 0, 1), 1.0)
    fill(a("Acol"), -31.0 / 64)
    fill(a("cp", 0, 32), 0.0)
    fill(a("cX", 0, 8), W)
    fill(a("Qf", W, W + 8), 0.0)
    fill(a("It", W, W + 8), 0.0)
    fill(a("eo", 8, 24), 0.0)
    fill(a("onf"), 1.0)
    fill(a("ce"), -1.0)
    ts(a("pJ", 0, 1), a("pI", 0, 1), 15, AND)
    cp(pcol, a("pI", 0, 1))
    cp(r16, a("pJ", 0, 1))
    tt(g16, a("pI", 0, 1), a("pJ", 0, 1), SUB)
    ts(a("pJ"), a("pI"), 7, AND)
    ts(hi, pcol, 64.0, GE, 64.0, MUL)
    scales = (1, -1)
    for j, c in enumerate(scales):
        ts(a("idn", 128 * j, 128 * j + 128), col, pcol, EQ, float(c), MUL)
    idn = {c: a("idn", 128 * j, 128 * j + 128) for j, c in enumerate(scales)}
    cp(a("l8"), a("pJ"))
    ts(npcol, pcol, -1.0, MUL, 1.0, ADD)
    ts(p16, pcol, 16.0, MUL)
    ts(kgt, r16, 1184.0, MUL, -2.0 ** 23, ADD)
    ts(r1, r16, 1.0, ADD)
    ts(g17, g16, 1.0, ADD)
    ts(sgn, hi, -1.0 / 64, MUL, 0.5, ADD)
    ts(p64, pcol, hi, SUB)
    ts(g64, g16, hi, SUB)
    ts(top64, hi, 64.0, SUB)
    ts(bot64, hi, -1.0, MUL)
    ts(robias, hi, (W + 128) / 64.0, MUL, r16, ADD)
    ts(g64b, g64, 64.0, ADD)
    ts(gsw, g64, top64, SUB)
    ts(a("cols", 16, 24), blk8, 0.125, MUL, -7.0, ADD)
    ts(a("sel"), a("tM"), gsw, EQ)
    ts(a("cols", 24, 32), a("cols", 16, 24), sgn, MUL, 0.5, ADD)
    for j, c in enumerate((2.0, -1.0, 1.0, top64, bot64)):
        ts(a("bdb", 8 * j, 8 * j + 8), blk8, g16, EQ, c, MUL)
    bd2, bdm1, bd1, bdtop, bdbot, bdw = (a("bdb", 8 * j, 8 * j + 8) for j in range(6))
    for j, c in enumerate((5, 6, 1, 2, 7, 0)):
        ts(a("Wl", 64 * j, 64 * j + 64), a("tM", 15, 79), p64, EQ, a("cols", 24 + c, 25 + c), MUL)
    ts(a("diag"), a("cu"), r16, EQ)
    ts(a("lhc"), a("cu"), p16, MUL, npcol, ADD)
    ts(a("eu"), blk8, g16, EQ, 2.0 ** 25, MUL)
    ts(a("ep"), a("tB"), g16, EQ, 32.0, MUL)
    cp(a("l11"), a("tI", 0, 8))
    cp(a("lg"), a("tI", 8, 16))
    ts(a("cp", 32, 72), a("tE", 0, 40), npcol, MUL, pcol, ADD)
    cp(a("R0"), a("Ri"))
    ts(a("bdf"), a("tA", 0, 128), g16, EQ)
    dk = a("tD")
    ts(dk, a("cu", 0, 16), r16, SUB)
    for j, (gg, c) in enumerate(((g64, 128.0), (g64b, 128.0), (g16, -128.0), (g64, 64.0), (g64b, 64.0), (g16, 64.0))):
        ts(a("bdh", 8 * j, 8 * j + 8), blk8, gg, EQ, c, MUL)
    ts(a("OH"), dk, 1.0, EQ)
    ts(a("ML"), dk, 0.0, GT, 32.0, MUL)
    ts(a("C3"), dk, -3.0, LT)
    ts(a("C4"), dk, 0.0, EQ, 32.0, MUL)
    ts(a("C1"), dk, 0.0, LT, 32.0, MUL)
    ts(a("C2"), dk, 0.0, GE, 65536.0, MUL)
    ts(a("tE", 48, 64), a("C3"), 2048.0, MUL)
    ts(a("tE", 64, 80), a("C3"), kgt, MUL)
    ts(a("KQ"), col, g16, EQ, r1, MUL)
    tt(a("C1"), a("C1"), a("tE", 48, 64), ADD)
    tt(a("C2"), a("C2"), a("tE", 64, 80), ADD)
    ts(a("KX"), col, g17, EQ, r1, MUL)
    ts(a("ybias"), r16, 0.0, EQ, 2048.0 * 136, MUL)
    ts(a("eo", 0, 8), blk8, g16, EQ, 128.0, MUL)
    ts(a("eo", 24, 32), blk8, g16, EQ, -128.0, MUL)
    ts(a("eg", 264, 272), blk8, g16, EQ, 8192.0, MUL)
    ts(a("nq"), a("tB", 0, 16), r16, ADD, 32.0, MUL)
    ts(a("wF"), a("wI", 0, 1), 2.0 ** -25, MUL)
    cp(a("kF"), a("kI", 0, 2))
    ts(bdw, blk8, g16, EQ, a("wF"), MUL)
    for h in range(2):
        ts(a("kh", 128 * h, 128 * h + 128), a("tA", 128, 256), r16, EQ, a("kF", h, h + 1), MUL)
    mm(a("pB", 0, 256), a("bdf"), a("kh"), True, True)

    def late_constants():
        ts(a("tE", 80, 97), a("tI", 16, 33), r16, ADD)
        ts(a("eg", 0, 264), a("tA", 256, 520), g16, EQ, -2.0 ** 20, MUL)
        ts(a("tJ", 0, 17), a("tE", 80, 97), 16.0, SUB, 1.0 / 33, MUL)
        ts(a("tE", 80, 97), a("tE", 80, 97), 8.0, MUL)
        ts(a("tE", 100, 117), a("tJ", 0, 17), -263.0, MUL)
        tt(a("tE", 80, 97), a("tE", 80, 97), a("tE", 100, 117), ADD)
        cp(a("lc", 0, 17), a("tE", 80, 97))
        keep(a("ce"), a("ce"), [[0, 8], [1, 33]], NE, 3.0e7, 0)
        iota(a("cm", 0, 264), [[0, 8], [-8192, 33]])
        iota(a("cm", 264, 272), [[0, 8]])
        iota(a("co"), [[4096, 2], [512, 8]])
        iota(a("It", 0, 1024), [[1, 1024]], -2048)

    Xw, Qw, Iw, Yw = a("X", 0, W), a("Qf"), a("It"), a("Y")
    WB = W + 128
    banks = BANKS
    y_back = [[0, 1, 2], [3, 4, 5], [6, 7]]
    y_bank = ("pA0", "pA1", "pA3")
    sent = 0

    def conv_q(lo, hi, q):
        if q == "S":
            act(a("Qf", lo, hi), a("Qi", lo, hi), bias=-2048.0)
        else:
            ts(a("Qf", lo, hi), a("Qi", lo, hi), 2048.0, SUB)

    def y_x(c, bank):
        mm(a(bank), a("KX"), a("X", 512 * c, 512 * c + 512), True, False)

    def y_q(c, bank):
        q16 = a("q16", 512 * (c % 3), 512 * (c % 3) + 512)
        act(q16, a("Qf", 512 * c, 512 * c + 512))
        mm(a(bank), a("KQ"), q16, False, True)

    def y_out(c, bank):
        act(a("Y", 512 * c, 512 * c + 512), a(bank), bias=a("ybias"))

    for v in range(VISITS):
        Rn = "R%d" % v
        if v:
            arrive(Rn, (rank - 1) % n_ranks, v - 1)
        mm(a("pD", 0, 128), zrow, a("cu", rows=1), True, False)
        mm(a("pU", 0, 128), r5, a("cu", rows=1), True, False)
        for h in range(2):
            cp(a("x", 1024 * h, 1024 * h + 512), ind(Xw, a(Rn, 64 * h, 64 * h + 32)))
            act(a("x", 1024 * h + 512, 1024 * h + 1024), ind(Xw, a(Rn, 64 * h + 32, 64 * h + 64)))
            for b, (k0, nk, who) in enumerate(banks):
                for j in range(nk if who == "S" else 0):
                    o = a("pA%d" % b, 128 * j + 64 * h, 128 * j + 64 * h + 64)
                    mm(o, idn[1], a("x", 1024 * h + k0 + j + 1, 1024 * h + 1024, 16), True, False)
                    mm(o, idn[-1], a("x", 1024 * h + k0 + j, 1024 * h + 1024, 16), False, True)
        if v:
            act(a("Yn"), a("pS", 0, 128), bias=a("ybias"))
            act(a("mb", 128, 256), a("pS", 128, 256))
            scatter(a("Qf", 0, W), a("n16", 0, 8), a("nF"))
        else:
            act(a("krep"), a("pB", 0, 256), bias=128.0)
            late_constants()
        for k0, nk, who in banks:
            for k in range(k0, k0 + nk):
                if who == "V":
                    mm(a("pD", k, 128, 16), a("x", k + 1, 2048, 16), bdm1, False, False)
                    mm(a("pD", k, 128, 16), a("x", k, 2048, 16), bdm1, False, False)
        for b, (k0, nk, who) in enumerate(banks):
            dst, src = a("ab", 128 * (k0 - 1), 128 * (k0 - 1 + nk)), a("pA%d" % b, 0, 128 * nk)
            if who == "V":
                for k in range(k0, k0 + nk):
                    tt(a("ab", 128 * (k - 1), 128 * k), a("x", k + 1, 2048, 16), a("x", k, 2048, 16), MAX)
            else:
                act(dst, src, ABS)
            for k in range(k0, k0 + nk):
                mm(a("pD", k, 128, 16), a("ab", 128 * (k - 1), 128 * k), bd2 if who == "V" else bd1, False, False)
        for k in range(1, 12):
            mm(a("pU", k, 128, 16), a("x", k, 2048, 16), bdw, False, False)
        mm(a("pD", 0, 8), zrow, a("cu", 0, 8, rows=1), False, True)
        mm(a("pU", 0, 8), zrow, a("cu", 0, 8, rows=1), False, True)
        if v == 0:
            for c in range(8 if F6 else 0):
                bank = ("pS", "pA3")[c % 2]
                for h in range(2):
                    mm(a(bank, half=h), a("idn", 64 - 64 * h, 128 - 64 * h), a("X", 512 * c, 512 * c + 512), True, True)
                (act if c % F6 else cp)(a("X", W + 512 * c, W + 512 * c + 512), a(bank))
            conv_q(0, 1024, "S")
            conv_q(1024, 2048, "S")
        if v:
            scatter(a("X", W, 2 * W), a("n16", 8, 16), a("mb", 128, 256))
        scan(a("run1"), a("pD", 0, 128), a("c1"), -1.0, MAX, MIN)
        tt(a("new", 1, 128), a("pD", 1, 128), a("run1", 0, 127), GT)
        mm(a("pD", 0, 72), a("lhc", rows=2), a("cp", rows=2), True, False)
        scan(a("sc3"), a("new"), a("pU", 0, 128), 0.0, MAX, MIN)
        tt(a("lhU"), ind(a("sc3"), a("l11")), a("diag"), MUL)
        mm(a("pB", 0, 8), a("lhU"), a("eu"), True, True)
        mm(a("pD", 0, 72), a("lhU"), a("ep"), False, True)
        for h in range(2):
            mm(a("pU", 0, 8, half=h), a("lhU", 64 - 64 * h, 128 - 64 * h), a("eu"), True, True)
        if v:
            scatter(Yw, a("n16", 0, 8), a("Yn"))
        cp(a("uP", 0, 8), a("pB", 0, 8))
        if F5:
            act(a("off"), a("pD", 0, 72), bias=-0.4961)
        else:
            ts(a("off"), a("pD", 0, 72), -0.4961, ADD)
        ts(a("uI"), a("uP", 0, 8), W - 1, AND)
        act(a("sq"), ind(a("uI"), a("l8", 0, 1)), SQUARE, bias=-2048.0)
        act(a("msk"), ind(a("OH"), a("off", 0, 32)))
        act(a("x5"), ind(a("x"), a("off", 32, 72)))

        def pairs():
            for j, (f, s) in enumerate(((2, 3), (1, 0))):
                xf_, xs_ = a("x5", 128 * f, 128 * f + 128), a("x5", 128 * s, 128 * s + 128)
                lo, up = a("idn", 0, 64), a("idn", 64, 128)
                for t, (w, first, second) in enumerate(((lo, xf_, xs_), (up, xs_, xf_))):
                    bank, c = ("pA1", "pA2")[j], 128 * t
                    mm(a(bank, c, c + 128, half=0), w, first, True, True)
                    mm(a(bank, c, c + 128, half=1), w, second, True, True)
            for j, c in enumerate((1, 1, -1)):
                mm(a("pA2", 256, 384), idn[c], a("x5", 256 + 128 * j, 384 + 128 * j), j == 0, j == 2)

        keep(a("t3", 1024, 1152), a("x5", 512, 640), [[0, 128]], GE, 0.0, 0)
        keep(a("t3", 1152, 1280), a("x5", 512, 640), [[0, 128]], GE, 0.0, 0)
        keep(a("t3", 1280, 1536), a("t3", 1024, 1280), [[0, 256]], GE, 0.0, 0)
        if v == 0:
            iota(a("It", 1024, W), [[1, W - 1024]], -1024)

        def c_list(lo, hi):
            tt(a("z1", lo, hi), ind(a("uI"), a("l8", 0, (hi - lo) // 16)), a("krep", lo, hi), MUL)
            if lo == 0:
                ts(a("sI"), a("sq", 0, 8), 1.0 / 32, MUL, a("Acol"), ADD)
            tt(a("zI", lo, hi), ind(a("sI"), a("l8", 0, (hi - lo) // 16)), a("z1", lo, hi), ADD)
            ts(a("cX", 8 + lo, 8 + hi), a("zI", lo, hi), W - 1, AND)
            (act if F2 and lo else cp)(a("c16", lo, hi), a("cX", 8 + lo, 8 + hi))

        def c_low(lo, hi):
            (act if F1 else cp)(a("b16", lo, hi, half=1), a("cX", 8 + lo, 8 + hi, half=1))

        c_list(0, 64)
        if v == 0:
            c_list(64, 256)
            conv_q(2048, 3072, "S")
            conv_q(3072, 3584, "V")
            conv_q(3584, W, "S")

        def q_sel(n):
            lo, s = 512 * n, n // 2
            tt(a("Qs", lo, lo + 512), ind(Qw, a("c16", lo // 16, lo // 16 + 32)), a("msk"), MUL)
            if HALF0 and n < 2:
                for r in range(16):
                    mm(a(("pB", "pS")[n], 0, 32), a("sel", 15 - r, 143 - r), a("Qs", lo + r, lo + 512, 16), r == 0, r == 15)
                act(a("c16", 32 * n, 32 * n + 32, half=1), a(("pB", "pS")[n], 0, 32, half=1), bias=2048.0 + W)
                act(a("b16", 32 * n, 32 * n + 32, half=0), a(("pB", "pS")[n], 0, 32, half=0), bias=2048.0 + W)
            elif n % 2:
                for r in range(16):
                    mm(a(("pB", "pU")[s % 2], 0, 64), a("sel", 15 - r, 143 - r), a("Qs", 1024 * s + r, 1024 * s + 1024, 16),
                       r == 0, r == 15)

        def b_list(s):
            pb = ("pB", "pU")[s % 2]
            if HALF0 and s == 0:
                pass
            elif s in B_ON_S:
                act(a("c16", 64 * s, 64 * s + 64, half=1), a(pb, 0, 64, half=1), bias=2048.0 + W)
                act(a("b16", 64 * s, 64 * s + 64, half=0), a(pb, 0, 64, half=0), bias=2048.0 + W)
            else:
                ts(a("c16", 64 * s, 64 * s + 64, half=1), a(pb, 0, 64, half=1), 2048.0 + W, ADD)
                ts(a("b16", 64 * s, 64 * s + 64, half=0), a(pb, 0, 64, half=0), 2048.0 + W, ADD)

        def x_ab(lo, n):
            for t, lst in enumerate(("c16", "b16")):
                act(a("AB", t * WB + 128 + lo, t * WB + 128 + lo + n), ind(a("X"), a(lst, lo // 16, (lo + n) // 16)))

        items = [(c, j) for c, j in ITEMS]
        ring = RING

        def span(c):
            return (128 + 512 * c, 512) if c < 8 else (0, 128)

        def line(n):
            c, j = items[n]
            lo, w = span(c)
            bank, abs_ = ring[n % len(ring)], c in ON_SCALAR
            ta, tb = a("AB", lo, lo + w), a("AB", WB + lo, WB + lo + w)
            if abs_:
                mm(a(bank, 0, w), idn[-1], a("t3", 512 * j, 512 * j + w), True, False)
            if j < 2:
                mm(a(bank, 0, w), a("Wl", 128 * j, 128 * j + 128), (ta, tb)[j], not abs_, True)
            else:
                mm(a(bank, 0, w, half=0), a("Wl", 256, 320), ta, not abs_, True)
                mm(a(bank, 0, w, half=1), a("Wl", 320, 384), tb, not abs_, True)

        def clip(n):
            c, j = items[n]
            lo, w = span(c)
            dst, src = a("Mx", j * WB + lo, j * WB + lo + w), a(ring[n % len(ring)], 0, w)
            if c in ON_SCALAR:
                act(dst, src, ABS)
            else:
                tt(dst, src, a("t3", 512 * j, 512 * j + w), MIN if j == 2 else MAX)

        def score(n):
            c, j = items[n]
            lo, w = span(c)
            abs_ = c in ON_SCALAR
            for m in range(lo, lo + w, 128):
                o = a("pS", m // 128, 264, 33)
                if abs_ and j == 0:
                    mm(o, a("tsum"), a("bdh", 40, 48), False, False)
                if not abs_ and j < 2:
                    mm(o, a("AB", j * WB + m, j * WB + m + 128), (bdtop, bdbot)[j], False, False)
                k = 8 * (j + 3 * abs_)
                mm(o, a("Mx", j * WB + m, j * WB + m + 128), a("bdh", k, k + 8), False, False)

        pl = a("off", 0, 8)
        c_low(0, 64)
        q_sel(0)
        pairs()
        for t in range(2):
            act(a("t3", 512 * t, 512 * t + 128), a("pA1", 128 * t, 128 * t + 128))
            keep(a("t3", 512 * t + 128, 512 * t + 256), a("t3", 512 * t, 512 * t + 128), [[0, 128]], GE, 0.0, 0)
            keep(a("t3", 512 * t + 256, 512 * t + 512), a("t3", 512 * t, 512 * t + 256), [[0, 256]], GE, 0.0, 0)
        x_ab(0, 512)
        q_sel(1)
        x_ab(512, 512)
        mm(a("pS", 0, 264), zrow, a("cg", 0, 264, rows=1), True, False)
        for t in range(2):
            act(a("AB", t * WB, t * WB + 128), a("pA2", 128 * t, 128 + 128 * t))
        act(a("tsum"), a("pA2", 256, 384))
        (act if F4 else cp)(a("uP", 8, 16), a("pU", 0, 8))
        if v:
            c_list(64, F3)
        q_sel(2)
        q_sel(3)
        if v and F3 < 256:
            c_list(F3, 256)
        c_low(64, 256)
        (act if F4 else cp)(a("Rf"), a(Rn))
        b_list(1)
        x_ab(1024, 1024)

        def tables():
            act(a("MLg"), ind(a("ML"), pl))
            act(a("Tt", 128, 256), a("Rf"), scale=32.0)
            mm(a("pB", 0, 272), r19, a("cg", rows=1), True, False)
            mm(a("pU", 0, 16), r5, a("co", rows=1), True, False)

        extra = {"T1": lambda: tt(a("T1"), ind(a("C1"), pl), a("Rf"), MUL),
                 "q4": lambda: q_sel(4), "q5": lambda: q_sel(5), "q6": lambda: q_sel(6), "q7": lambda: q_sel(7),
                 "b2": lambda: b_list(2), "b3": lambda: b_list(3),
                 "x2": lambda: x_ab(2048, 1024), "x3": lambda: x_ab(3072, 1024), "tab": tables,
                 "ct": lambda: tt(a("ctab"), ind(a("cX"), a("lc", 0, 17)), a("cm"), ADD),
                 "M1": lambda: tt(a("M1"), ind(a("C3"), pl), a("Rf"), MUL),
                 "Tt": lambda: tt(a("Tt", 0, 128), ind(a("C2"), pl), a("T1"), ADD),
                 "MM": lambda: tt(a("MM"), ind(a("C4"), pl), a("M1"), ADD)}
        for n in range(AHEAD):
            line(n)
        for n in range(len(items)):
            clip(n)
            for e in AFTER.get(n, ()):
                extra[e]()
            if n + AHEAD < len(items):
                line(n + AHEAD)
            score(n)
        mm(a("pS", 0, 8), zrow, a("cu", 0, 8, rows=1), False, True)
        scan(a("runE"), a("ce"), a("pS", 0, 264), 0.0, ADD, MIN)
        ts(a("mP"), a("runE", 32, 264, 33), 6291488.0, ADD)
        ts(a("mI"), a("mP"), 63, AND)
        tt(a("lhM"), ind(a("mI"), a("lg")), a("diag"), MUL)
        mm(a("pB", 0, 272), a("lhM"), a("eg"), False, True)
        act(a("lhS"), a("lhM"), SIGN, acc=a("cnt"))
        mm(a("pU", 0, 16), a("lhM"), a("eo", 0, 16), False, False)
        mm(a("pU", 0, 16), a("lhS"), a("eo", 16, 32), False, True)
        act(a("l16", 16, 24), a("pU", 8, 16), bias=r16)
        act(a("l16", 8, 16), a("pU", 0, 8), bias=robias)
        mb = a("mb", 0, 128)
        act(a("ms"), ind(a("AB"), a("l16", 8, 16)))
        mm(a("pA2", 0, 128), idn[1], a("x5", 256, 384), True, False)
        mm(a("pA2", 0, 128), idn[1], a("ms"), False, True)
        act(a("mf"), a("pA2", 0, 128), bias=-0.25, scale=0.5)
        act(mb, a("mf"))
        ts(a("n1"), a("uP"), 31, AND)
        tt(a("n2"), a("n1"), a("nq"), ADD)
        cp(a("n16"), a("n2"))
        scan(a("runG"), a("pB", 0, 264), a("ctab", 0, 264), 0.0, MIN, MAX)
        tt(a("lf", 0, 8), a("pB", 264, 272), a("runG", 32, 264, 33), ADD)
        cp(a("l16", 0, 8), a("lf", 0, 8))
        last = v + 1 == VISITS
        for j, c in enumerate(y_back[v]):
            y_x(c, y_bank[j])
        if not last:
            mm(a("pD", 0, 1), a("onf"), a("cnt"), True, True)
            act(a("Acol"), a("pD", 0, 1), bias=-31.0 / 64)
        for j, c in enumerate(y_back[v]):
            y_q(c, y_bank[j])
            y_out(c, y_bank[j])
        cl = a("l16", 0, 8)
        tt(a("h2"), ind(Qw, cl), a("MLg"), MUL)
        tt(a("h1"), ind(Iw, cl), a("MM"), MUL)
        tt(a("h3"), ind(a("Tt"), a("l16", 16, 24)), a("h2"), ADD)
        tt(a("h4"), a("h1"), a("h3"), ADD)
        ts(a("nI"), a("h4"), 5, SHR, W - 1, AND)
        cp(a("S%d" % v), a("nI"))
        sent += send(a("S%d" % v), "Rfin" if last else "R%d" % (v + 1), (rank - v if last else rank + 1) % n_ranks, v)
        act(a("nF"), a("nI"), bias=-2048.0)
        mm(a("pS", 0, 128), a("KQ"), a("nF"), True, False)
        mm(a("pS", 0, 128), a("KX"), mb, False, True)
        if not last:
            for h in range(2):
                mm(a("pS", 128, 256, half=h), a("idn", 64 - 64 * h, 128 - 64 * h), mb, True, True)
            scatter(Xw, a("n16", 0, 8), mb)

    act(a("Yn"), a("pS", 0, 128), bias=a("ybias"))
    scatter(Yw, a("n16", 0, 8), a("Yn"))
    dma("Y", T.yq[:, :], (T.Y[0:128:16, :], Yw[1]), "stQ", 1 << 17)
    dma("S", T.yx[:, :], (T.Y[1:128:16, :], Yw[1]), "stX", 1 << 17)
    arrive("Rfin", (rank + VISITS - 1) % n_ranks, VISITS - 1)
    dma("Y", T.yr[:, :], a("Rfin"), "stR", 1 << 16)

    def meet(x, y):
        return any(p[0] == s[0] and (p[0] in _PS or (p[1] < s[2] and s[1] < p[2] and p[3] < s[4] and s[3] < p[4]))
                   for p in x for s in y)

    def psum(o):
        return [r for r in o["r"] + o["w"] if r[0] in _PS]

    def clash(e, o):
        if e["q"] == o["q"] == "P":
            return meet(e["w"], o["w"]) and not (e["adds"] and o["adds"])
        return meet(e["w"], o["r"]) or meet(e["w"], o["w"]) or meet(e["r"], o["w"]) or (e["q"] != o["q"] and meet(psum(e), psum(o)))

    if not _ORDER:
        _ORDER.extend(plan(ops, clash))
    ops = [ops[n] for n in _ORDER]
    known = {q: {} for q in Q}
    by_name = {}
    for n, o in enumerate(ops):
        o["waits"], o["need"] = [], False
        own = o["sem"] is not None
        o["key"] = o["sem"] if own else o["q"]
        if len(_WAITS) == len(ops):
            o["waits"] = _WAITS[n]
            for m in o["waits"]:
                ops[m]["need"] = True
            continue
        if o["q"] is not None:
            names = {r[0] for r in o["r"] + o["w"]}
            cand = sorted({m for nm in names for m in by_name.get(nm, [])}, reverse=True)
            kn = known[o["q"]]
            for m in cand:
                e = ops[m]
                if e["key"] == "remote" or kn.get(e["key"], -1) >= m:
                    continue
                dep = meet(e["w"], o["r"]) or meet(e["w"], o["w"]) or meet(e["r"], o["w"])
                if e["key"] == o["q"] and not own:
                    dep = dep and o["q"] != "P"
                else:
                    dep = dep or meet(psum(e), psum(o))
                if dep:
                    o["waits"].append(m)
                    e["need"] = True
                    kn[e["key"]] = m
                    for kk, mm_ in e["clock"].items():
                        kn[kk] = max(kn.get(kk, -1), mm_)
            o["clock"] = dict(kn)
        else:
            o["clock"] = {}
        for nm in {r[0] for r in o["r"] + o["w"]}:
            by_name.setdefault(nm, []).append(n)
    _WAITS[:] = [o["waits"] for o in ops]
    count = {q: 0 for q in Q}
    for o in ops:
        if o["sem"] is None and o["need"]:
            count[o["q"]] += 1
            o["inc"], o["sem"], o["val"] = 1, "c" + o["q"], count[o["q"]]
        else:
            o["inc"] = 16 if (o["q"] is not None and o["sem"] not in (None, "remote")) else 0
    for o in ops:
        if o["q"] is None:
            continue
        for m in o["waits"]:
            Q[o["q"]].wait_ge(T.sem[ops[m]["sem"]], ops[m]["val"])
        ins = o["fn"]()
        if o["inc"]:
            ins.then_inc(T.sem[o["sem"]], o["inc"])
    g.wait_ge(T.sem.sent, sent)
    for s in ("stQ", "stX", "stR"):
        g.wait_ge(T.sem[s], 16)
